import numpy as np
import ml_dtypes


def mxq(x, axis, fmt="e4m3"):
    dtype, down = {"e4m3": (ml_dtypes.float8_e4m3fn, 7), "e5m2": (ml_dtypes.float8_e5m2, 14)}[fmt]
    v = np.moveaxis(np.asarray(x, np.float32).astype(ml_dtypes.bfloat16).astype(np.float64), axis, -1)
    blocks = v.reshape(v.shape[:-1] + (-1, 32))
    amax = np.abs(blocks).max(-1, keepdims=True)
    byte = np.maximum(np.where(amax > 0, np.frexp(amax)[1] - 1 + 127, 0) - down, 1)
    scale = np.exp2(byte - 127.0)
    codes = (blocks / scale).astype(np.float32).astype(dtype).astype(np.float64)
    return np.moveaxis((codes * scale).reshape(v.shape), -1, axis)


WIDE = False


def mx_kscale(k):
    if not WIDE:
        return np.ones(k)
    levels = np.array([10, -10, 5, -5, 0])
    if k % 512:
        return np.exp2(np.random.permutation(np.resize(levels, k // 32))).repeat(32)
    a = np.empty((k // 512, 16))
    for p in range(k // 512):
        a[p, :8] = np.random.permutation(np.resize(levels, 8))
        for g in range(8):
            far = levels[np.abs(levels - a[p, g]) >= 10]
            a[p, g + 8] = far[np.random.randint(len(far))]
    return np.exp2(a.ravel()).repeat(32)


BF16 = ml_dtypes.bfloat16


def bf(x):
    return np.asarray(x, np.float32).astype(BF16)


def f64(x):
    return np.asarray(x).astype(np.float64)


T, D, F, R = 1024, 1024, 1024, 512


def hadamard_delta(p1, p2):
    return 0.05 * np.tanh(p1) * (1.0 + np.tanh(p2))


def draw0():
    s = mx_kscale(D)
    a, b = mx_kscale(R), mx_kscale(R)
    return {
        "x": bf(np.random.standard_normal((T, D)) / s[None, :]),
        "w0": bf(np.random.standard_normal((D, F)) / np.sqrt(D)),
        "x1": bf(np.random.standard_normal((D, R)) * a[None, :]),
        "y1": bf(np.random.standard_normal((R, F)) / np.sqrt(R) / a[:, None]),
        "x2": bf(np.random.standard_normal((D, R)) * b[None, :]),
        "y2": bf(np.random.standard_normal((R, F)) / np.sqrt(R) / b[:, None]),
        "gain": bf((1.0 + 0.1 * np.random.standard_normal(D)) * s),
    }


def core(x, w0, x1, y1, x2, y2, gain):
    p1 = mxq(f64(x1), 1, "e4m3") @ mxq(f64(y1), 0, "e4m3")
    p2 = mxq(f64(x2), 1, "e4m3") @ mxq(f64(y2), 0, "e4m3")
    dw = hadamard_delta(p1, p2)
    w = f64(gain)[:, None] * (f64(w0) + dw)
    return mxq(f64(x), 1, "e4m3") @ mxq(w, 0, "e4m3")


def e4m3fn_bytes(y):
    return np.clip(np.asarray(y, np.float64), -448.0, 448.0).astype(np.float32).astype(ml_dtypes.float8_e4m3fn).view(np.uint8)


def e4m3fn_values(b):
    return np.asarray(b, np.uint8).view(ml_dtypes.float8_e4m3fn).astype(np.float64)


def setup_inputs():
    d = draw0()
    x0 = np.asarray(d['x']).astype(np.float64)
    s = (np.max(np.abs(x0), axis=(0,), keepdims=True) / 448.0).astype(np.float32)
    out = {}
    for k, v in d.items():
        if k == 'x':
            out['x_bytes'] = e4m3fn_bytes(x0 / s.astype(np.float64))
            out['x_scale'] = s
        else:
            out[k] = v
    return out


def reference(x_bytes, x_scale, w0, x1, y1, x2, y2, gain):
    return core(e4m3fn_values(x_bytes) * x_scale.astype(np.float64), w0, x1, y1, x2, y2, gain)

@@ -1,0 +1,587 @@
+from contextlib import ExitStack
+
+import concourse.mybir as mybir
+from concourse.masks import make_identity
+
+T, D, F, R = 1024, 1024, 1024, 512
+FLOPS = 2 * 2 * D * R * F + 2 * T * D * F
+
+F32 = mybir.dt.float32
+BF16 = mybir.dt.bfloat16
+U32 = mybir.dt.uint32
+U8 = mybir.dt.uint8
+FP8 = mybir.dt.float8_e4m3fn
+FP8X4 = mybir.dt.float8_e4m3fn_x4
+ACT = mybir.ActivationFunctionType
+ALU = mybir.AluOpType
+
+WD = {0: 512, 512: 256, 768: 256}
+
+
+def tile_fedparatanhhadamardlinear_kernel(
+    tc, x_bytes, x_scale, w0, x1, y1, x2, y2, gain, out
+):
+    nc = tc.nc
+    with ExitStack() as ctx:
+        keep = ctx.enter_context(tc.tile_pool(name="keep", bufs=1))
+        work = ctx.enter_context(tc.tile_pool(name="work", bufs=2))
+        psum = ctx.enter_context(tc.psum_pool(name="psum", bufs=8))
+        ctx.enter_context(
+            tc.manual_schedule(
+                engines={
+                    mybir.EngineType.PE,
+                    mybir.EngineType.Activation,
+                    mybir.EngineType.DVE,
+                }
+            )
+        )
+
+        def bank():
+            b = psum.tile([128, 512], F32, name="bank", tag="bank")
+            return b
+
+        def take(eng, dst, src):
+            if eng == "S":
+                nc.scalar.copy(dst, src)
+            else:
+                nc.vector.tensor_copy(out=dst, in_=src)
+
+        warm = keep.tile([128, 1], F32, name="warm")
+        nc.vector.memset(warm[:], 0.0)
+        nc.scalar.activation(warm[:], warm[:], ACT.Sigmoid)
+        ident = keep.tile([128, 128], F32, name="ident")
+        make_identity(nc, ident[:])
+        identb = keep.tile([128, 128], BF16, name="identb")
+        make_identity(nc, identb[:])
+
+        gain_bf = keep.tile([128, 8], BF16, name="gain_bf")
+        nc.scalar.dma_start(
+            out=gain_bf[:].rearrange("p (g t) -> p g t", g=2),
+            in_=gain.rearrange("(g p t) -> p g t", g=2, p=128, t=4),
+        )
+        xs_t = keep.tile([128, 1024], F32, name="xs_t")
+        y_raw = {}
+        xr = {}
+        w0_raw = {}
+        xb = {}
+
+        def load_sc():
+            nc.sync.dma_start(
+                out=xs_t[:], in_=x_scale.rearrange("o k -> (o k)").partition_broadcast(128)
+            )
+
+        def load_y(w, h):
+            y = y1 if w == 0 else y2
+            t = keep.tile([128, 4, 512], BF16, name="y%d%d" % (w, h))
+            nc.sync.dma_start(
+                out=t[:],
+                in_=y.rearrange("(p j) f -> p j f", j=4)[:, :, 512 * h : 512 * h + 512],
+            )
+            y_raw[w, h] = t
+
+        def load_x12(w, g):
+            x = x1 if w == 0 else x2
+            t = keep.tile([128, 4, 512], BF16, name="x%d%d" % (w, g))
+            nc.sync.dma_start(
+                out=t[:],
+                in_=x.rearrange("(g m t) k -> g m t k", g=2, m=128, t=4)[g],
+            )
+            xr[w, g] = t
+
+        def load_w0(g, h):
+            t = keep.tile([128, 4, 512], BF16, name="w%d%d" % (g, h))
+            nc.sync.dma_start(
+                out=t[:],
+                in_=w0.rearrange("(g m t) f -> g m t f", g=2, m=128, t=4)[
+                    g, :, :, 512 * h : 512 * h + 512
+                ],
+            )
+            w0_raw[g, h] = t
+
+        def load_x(half):
+            t = keep.tile([128, 4, 1024], U8, name="xb%d" % half)
+            nc.sync.dma_start(
+                out=t[:],
+                in_=x_bytes.rearrange("(h i p) d -> h p i d", h=2, i=4, p=128)[half],
+            )
+            xb[half] = t
+
+        load_y(0, 0)
+        load_x12(0, 0)
+        load_y(1, 0)
+        load_x12(1, 0)
+        load_sc()
+        load_x(0)
+        load_x12(0, 1)
+        load_x12(1, 1)
+        load_w0(0, 0)
+        load_w0(1, 0)
+        load_x(1)
+        load_y(0, 1)
+        load_y(1, 1)
+        load_w0(0, 1)
+        load_w0(1, 1)
+
+        x12c = keep.tile([128, 4, 512], U32, name="x12c", align_bytes=256)
+        x12s = keep.tile([128, 4, 512], U8, name="x12s", align_bytes=256)
+        yc = keep.tile([128, 2, 1024], U32, name="yc", align_bytes=256)
+        ys = keep.tile([128, 2, 1024], U8, name="ys", align_bytes=256)
+        xc = keep.tile([128, 2, 1024], U32, name="xc", align_bytes=256)
+        xsc = keep.tile([128, 2, 1024], U8, name="xsc", align_bytes=256)
+        wc = keep.tile([128, 2, 1024], U32, name="wc", align_bytes=256)
+        ws = keep.tile([128, 2, 1024], U8, name="ws", align_bytes=256)
+
+        gain_f = keep.tile([128, 8], F32, name="gain_f")
+        gain_1 = keep.tile([128, 8], F32, name="gain_1")
+        diag = keep.tile([128, 8, 128], BF16, name="diag")
+
+        def prep_gain():
+            nc.vector.tensor_copy(out=gain_f[:], in_=gain_bf[:])
+            nc.vector.tensor_scalar(
+                out=gain_1[:], in0=gain_bf[:], scalar1=0.1, scalar2=None, op0=ALU.mult
+            )
+            for j in range(8):
+                nc.vector.tensor_scalar(
+                    out=diag[:, j, :],
+                    in0=identb[:],
+                    scalar1=gain_f[:, j : j + 1],
+                    scalar2=None,
+                    op0=ALU.mult,
+                )
+
+        xt12 = {}
+        banks = {}
+
+        def turn_x12(w, g, b):
+            words = xr[w, g][:].rearrange("p t k -> p (t k)").bitcast(F32)
+            pb = bank()
+            for tt in range(2):
+                for u in range(2):
+                    o = 256 * (2 * b + tt)
+                    nc.tensor.transpose(
+                        pb[:, 256 * tt + 128 * u : 256 * tt + 128 * u + 128],
+                        words[:, o + u : o + 256 : 2],
+                        ident[:],
+                    )
+            banks["x12", w, g, b] = pb
+
+        def take_x12(w, g, b, eng):
+            if (w, g) not in xt12:
+                t = work.tile([128, 2048], BF16, name="xt12", tag="xt12", bufs=4, align_bytes=256)
+                xt12[w, g] = t
+            take(
+                eng,
+                xt12[w, g][:]
+                .bitcast(F32)[:, 512 * b : 512 * b + 512]
+                .rearrange("p (t m u) -> p t m u", t=2, m=128),
+                banks["x12", w, g, b][:].rearrange("p (t u m) -> p t m u", t=2, u=2),
+            )
+
+        def quant_x12(w, g):
+            nc.vector.quantize_mx(
+                out=x12c[:, 2 * w + g, :].bitcast(FP8X4),
+                scales=x12s[:, 2 * w + g, :],
+                in_=xt12[w, g][:],
+            )
+
+        yg = {}
+
+        def new_yg(w, h):
+            if (w, h) not in yg:
+                t = work.tile([128, 512, 4], BF16, name="yg", tag="yg", bufs=3, align_bytes=256)
+                yg[w, h] = t
+            return yg[w, h]
+
+        def lay_y(w, h):
+            t = new_yg(w, h)
+            nc.vector.tensor_copy(out=t[:], in_=y_raw[w, h][:].rearrange("p j f -> p f j"))
+
+        def turn_y(w, h, b):
+            pb = psum.tile([128, 1024], BF16, name="bank", tag="bank")
+            for a in range(2):
+                n = 256 * b + 128 * a
+                nc.tensor.matmul(
+                    pb[:, 512 * a : 512 * a + 512],
+                    lhsT=identb[:],
+                    rhs=y_raw[w, h][:, :, n : n + 128].rearrange("p j n -> p n j"),
+                    start=True,
+                    stop=True,
+                )
+            banks["y", w, h, b] = pb
+
+        def take_y(w, h, b, eng):
+            t = new_yg(w, h)
+            take(
+                eng,
+                t[:].rearrange("p f j -> p (f j)").bitcast(F32)[:, 512 * b : 512 * b + 512],
+                banks["y", w, h, b][:].bitcast(F32),
+            )
+
+        def quant_y(w, h):
+            nc.vector.quantize_mx(
+                out=yc[:, w, 512 * h : 512 * h + 512].bitcast(FP8X4),
+                scales=ys[:, w, 512 * h : 512 * h + 512],
+                in_=yg[w, h][:].rearrange("p f j -> p (f j)"),
+            )
+
+        xw = {}
+        xt = {}
+
+        def scale_x(i):
+            t = work.tile([128, 1024], BF16, name="xw", tag="xw", bufs=4, align_bytes=256)
+            nc.vector.tensor_tensor(
+                out=t[:], in0=xb[i // 4][:, i % 4, :].bitcast(FP8), in1=xs_t[:], op=ALU.mult
+            )
+            xw[i] = t
+
+        def turn_x(i):
+            words = xw[i][:].bitcast(F32)
+            pb = bank()
+            for g in range(2):
+                for u in range(2):
+                    o = 256 * g + 128 * u
+                    nc.tensor.transpose(
+                        pb[:, o : o + 128], words[:, 256 * g + u : 256 * g + 256 : 2], ident[:]
+                    )
+            banks["x", i] = pb
+
+        def take_x(i, eng):
+            half = i // 4
+            if half not in xt:
+                t = work.tile([128, 2, 2048], BF16, name="xt", tag="xt", bufs=2, align_bytes=256)
+                xt[half] = t
+            r = 256 * (i % 4)
+            take(
+                eng,
+                xt[half][:]
+                .bitcast(F32)[:, :, r : r + 256]
+                .rearrange("p g (r u) -> p g r u", u=2),
+                banks["x", i][:].rearrange("p (g u r) -> p g r u", g=2, u=2),
+            )
+
+        def quant_x(half, g):
+            nc.vector.quantize_mx(
+                out=xc[:, g, 512 * half : 512 * half + 512].bitcast(FP8X4),
+                scales=xsc[:, g, 512 * half : 512 * half + 512],
+                in_=xt[half][:, g, :],
+            )
+
+        pt = {}
+
+        def mm_p(w, g, f0, wd, j):
+            per = 512 // wd
+            pb = bank()
+            for a in range(per):
+                t = j * per + a
+                nc.tensor.matmul_mx(
+                    out=pb[:, a * wd : (a + 1) * wd],
+                    lhsT=x12c[:, 2 * w + g, 128 * t : 128 * t + 128].bitcast(FP8X4),
+                    lhsT_scale=x12s[:, 2 * w + g, 128 * t : 128 * t + 128],
+                    rhs=yc[:, w, f0 : f0 + wd].bitcast(FP8X4),
+                    rhs_scale=ys[:, w, f0 : f0 + wd],
+                    start=True,
+                    stop=True,
+                )
+            banks["p", w, g, f0, j] = pb
+
+        def act_p(w, g, f0, wd, j):
+            pb = banks["p", w, g, f0, j]
+            if w == 0:
+                a = work.tile([128, 512], F32, name="t1", tag="t1", bufs=6)
+                nc.scalar.activation(a[:], pb[:], ACT.Tanh)
+            else:
+                a = work.tile([128, 512], F32, name="s2", tag="s2", bufs=6)
+                nc.scalar.activation(a[:], pb[:], ACT.Sigmoid, scale=2.0)
+            pt[w, g, f0, j] = a
+
+        qt = {}
+        wb = {}
+
+        def mul_q(g, f0, wd, j):
+            per = 512 // wd
+            if (g, f0) not in qt:
+                q = work.tile([128, 4, wd], F32, name="qt", tag="qt", bufs=3)
+                qt[g, f0] = q
+            for a in range(per):
+                t = j * per + a
+                sl = slice(a * wd, (a + 1) * wd)
+                nc.vector.scalar_tensor_tensor(
+                    out=qt[g, f0][:, t, :],
+                    in0=pt[0, g, f0, j][:, sl],
+                    scalar=gain_1[:, 4 * g + t : 4 * g + t + 1],
+                    in1=pt[1, g, f0, j][:, sl],
+                    op0=ALU.mult,
+                    op1=ALU.mult,
+                )
+
+        def mm_g(g, f0, wd, n):
+            pb = bank()
+            o = f0 % 512 + 128 * n
+            for t in range(4):
+                nc.tensor.matmul(
+                    pb[:, 128 * t : 128 * t + 128],
+                    lhsT=diag[:, 4 * g + t, :],
+                    rhs=w0_raw[g, f0 // 512][:, t, o : o + 128],
+                    start=True,
+                    stop=True,
+                )
+            banks["g", g, f0, n] = pb
+
+        def add_w(g, f0, wd, n):
+            if (g, f0) not in wb:
+                t = work.tile([128, 4 * wd], BF16, name="wb", tag="wb", bufs=3, align_bytes=256)
+                wb[g, f0] = t
+            nc.vector.tensor_tensor(
+                out=wb[g, f0][:, 512 * n : 512 * n + 512].rearrange("p (n t) -> p n t", t=4),
+                in0=banks["g", g, f0, n][:].rearrange("p (t n) -> p n t", t=4),
+                in1=qt[g, f0][:, :, 128 * n : 128 * n + 128].rearrange("p t n -> p n t"),
+                op=ALU.add,
+            )
+
+        def quant_w(g, f0, wd):
+            nc.vector.quantize_mx(
+                out=wc[:, g, f0 : f0 + wd].bitcast(FP8X4),
+                scales=ws[:, g, f0 : f0 + wd],
+                in_=wb[g, f0][:],
+            )
+
+        def mm_out(f0, wd, k):
+            per = 512 // wd
+            pb = bank()
+            for a in range(per):
+                i = k * per + a
+                for g in range(2):
+                    nc.tensor.matmul_mx(
+                        out=pb[:, a * wd : (a + 1) * wd],
+                        lhsT=xc[:, g, 128 * i : 128 * i + 128].bitcast(FP8X4),
+                        lhsT_scale=xsc[:, g, 128 * i : 128 * i + 128],
+                        rhs=wc[:, g, f0 : f0 + wd].bitcast(FP8X4),
+                        rhs_scale=ws[:, g, f0 : f0 + wd],
+                        start=(g == 0),
+                        stop=(g == 1),
+                    )
+            banks["o", f0, k] = pb
+
+        def take_out(f0, wd, k, eng):
+            per = 512 // wd
+            o = work.tile([128, per, wd], F32, name="o", tag="o", bufs=6)
+            take(eng, o[:].rearrange("p a f -> p (a f)"), banks["o", f0, k][:])
+            nc.sync.dma_start(
+                out=out.rearrange("(k a p) f -> k p a f", a=per, p=128)[k, :, :, f0 : f0 + wd],
+                in_=o[:],
+            )
+
+        pass
+        lay_y(0, 0)
+        turn_x12(0, 0, 1)
+        turn_x12(0, 0, 0)
+        quant_y(0, 0)
+        take_x12(0, 0, 1, "S")
+        lay_y(1, 0)
+        take_x12(0, 0, 0, "S")
+        turn_x12(1, 0, 1)
+        quant_x12(0, 0)
+        turn_x12(1, 0, 0)
+        take_x12(1, 0, 1, "S")
+        quant_y(1, 0)
+        mm_p(0, 0, 0, WD[0], 2)
+        take_x12(1, 0, 0, "S")
+        mm_p(0, 0, 0, WD[0], 0)
+        act_p(0, 0, 0, WD[0], 2)
+        mm_p(0, 0, 0, WD[0], 3)
+        quant_x12(1, 0)
+        prep_gain()
+        mm_p(0, 0, 0, WD[0], 1)
+        act_p(0, 0, 0, WD[0], 3)
+        scale_x(1)
+        mm_p(1, 0, 0, WD[0], 1)
+        act_p(0, 0, 0, WD[0], 0)
+        mm_p(1, 0, 0, WD[0], 0)
+        turn_x12(0, 1, 1)
+        act_p(1, 0, 0, WD[0], 1)
+        scale_x(3)
+        turn_x(1)
+        act_p(1, 0, 0, WD[0], 0)
+        mm_p(1, 0, 0, WD[0], 2)
+        act_p(0, 0, 0, WD[0], 1)
+        mul_q(0, 0, WD[0], 0)
+        turn_x12(1, 1, 0)
+        act_p(1, 0, 0, WD[0], 2)
+        scale_x(0)
+        mm_g(0, 0, WD[0], 2)
+        take_x(1, "S")
+        mm_p(1, 0, 0, WD[0], 3)
+        turn_x12(0, 1, 0)
+        take_x12(0, 1, 1, "S")
+        mul_q(0, 0, WD[0], 1)
+        act_p(1, 0, 0, WD[0], 3)
+        mm_g(1, 0, WD[0], 0)
+        mul_q(0, 0, WD[0], 2)
+        mm_g(1, 0, WD[0], 1)
+        take_x12(0, 1, 0, "S")
+        scale_x(6)
+        turn_x12(1, 1, 1)
+        take_x12(1, 1, 0, "S")
+        turn_x(0)
+        take_x12(1, 1, 1, "S")
+        quant_x12(0, 1)
+        turn_y(0, 1, 1)
+        take_x(0, "S")
+        scale_x(5)
+        turn_y(0, 1, 0)
+        take_y(0, 1, 1, "S")
+        mm_p(0, 1, 0, WD[0], 3)
+        quant_x12(1, 1)
+        take_y(0, 1, 0, "S")
+        turn_y(1, 1, 1)
+        act_p(0, 1, 0, WD[0], 3)
+        scale_x(4)
+        mm_g(0, 512, WD[512], 0)
+        mm_p(1, 1, 0, WD[0], 2)
+        take_y(1, 1, 1, "S")
+        mm_p(1, 1, 0, WD[0], 1)
+        mm_p(1, 1, 0, WD[0], 3)
+        act_p(1, 1, 0, WD[0], 2)
+        quant_y(0, 1)
+        mm_p(1, 1, 0, WD[0], 0)
+        act_p(1, 1, 0, WD[0], 3)
+        mul_q(0, 0, WD[0], 3)
+        turn_x(4)
+        act_p(1, 1, 0, WD[0], 1)
+        scale_x(2)
+        mm_p(0, 1, 512, WD[512], 1)
+        take_x(4, "S")
+        mm_g(1, 0, WD[0], 2)
+        act_p(1, 1, 0, WD[0], 0)
+        add_w(0, 0, WD[0], 2)
+        mm_p(0, 1, 0, WD[0], 1)
+        act_p(0, 1, 512, WD[512], 1)
+        mul_q(1, 0, WD[0], 3)
+        turn_x(2)
+        act_p(0, 1, 0, WD[0], 1)
+        scale_x(7)
+        mm_g(0, 0, WD[0], 1)
+        take_x(2, "S")
+        mm_p(0, 1, 0, WD[0], 0)
+        mm_p(0, 1, 0, WD[0], 2)
+        add_w(0, 0, WD[0], 1)
+        act_p(0, 1, 0, WD[0], 0)
+        mm_g(0, 0, WD[0], 3)
+        mul_q(1, 0, WD[0], 1)
+        act_p(0, 1, 0, WD[0], 2)
+        turn_x(7)
+        mul_q(1, 0, WD[0], 0)
+        turn_y(1, 1, 0)
+        take_x(7, "S")
+        mul_q(1, 0, WD[0], 2)
+        turn_x(3)
+        take_y(1, 1, 0, "S")
+        add_w(0, 0, WD[0], 3)
+        turn_x(6)
+        add_w(1, 0, WD[0], 0)
+        take_x(3, "S")
+        mm_g(0, 0, WD[0], 0)
+        quant_y(1, 1)
+        take_x(6, "S")
+        mm_p(0, 0, 512, WD[512], 1)
+        mm_p(0, 0, 512, WD[512], 0)
+        quant_x(0, 0)
+        act_p(0, 0, 512, WD[512], 1)
+        mm_p(1, 1, 512, WD[512], 1)
+        mm_p(1, 0, 768, WD[768], 0)
+        add_w(0, 0, WD[0], 0)
+        act_p(1, 1, 512, WD[512], 1)
+        mm_p(1, 0, 512, WD[512], 0)
+        quant_x(0, 1)
+        mm_p(1, 0, 768, WD[768], 1)
+        act_p(1, 0, 768, WD[768], 0)
+        mm_g(1, 0, WD[0], 3)
+        add_w(1, 0, WD[0], 1)
+        act_p(0, 0, 512, WD[512], 0)
+        mm_g(1, 512, WD[512], 1)
+        add_w(1, 0, WD[0], 3)
+        turn_x(5)
+        act_p(1, 0, 512, WD[512], 0)
+        add_w(1, 0, WD[0], 2)
+        act_p(1, 0, 768, WD[768], 1)
+        mm_g(0, 512, WD[512], 1)
+        mul_q(0, 512, WD[512], 0)
+        mm_p(1, 0, 512, WD[512], 1)
+        take_x(5, "S")
+        mm_p(0, 1, 768, WD[768], 0)
+        quant_w(0, 0, WD[0])
+        mm_p(0, 1, 512, WD[512], 0)
+        act_p(1, 0, 512, WD[512], 1)
+        mm_p(0, 0, 768, WD[768], 0)
+        quant_x(1, 0)
+        mm_p(0, 1, 768, WD[768], 1)
+        act_p(0, 1, 512, WD[512], 0)
+        mm_g(1, 768, WD[768], 1)
+        mul_q(0, 512, WD[512], 1)
+        act_p(0, 1, 768, WD[768], 1)
+        mm_g(1, 768, WD[768], 0)
+        quant_x(1, 1)
+        act_p(0, 0, 768, WD[768], 0)
+        mm_p(1, 1, 512, WD[512], 0)
+        add_w(0, 512, WD[512], 0)
+        act_p(0, 1, 768, WD[768], 0)
+        mm_g(0, 768, WD[768], 1)
+        add_w(0, 512, WD[512], 1)
+        act_p(1, 1, 512, WD[512], 0)
+        mm_p(0, 0, 768, WD[768], 1)
+        mm_p(1, 1, 768, WD[768], 1)
+        quant_w(1, 0, WD[0])
+        act_p(0, 0, 768, WD[768], 1)
+        mm_p(1, 1, 768, WD[768], 0)
+        mm_g(1, 512, WD[512], 0)
+        mul_q(1, 512, WD[512], 0)
+        act_p(1, 1, 768, WD[768], 1)
+        mm_g(0, 768, WD[768], 0)
+        mul_q(0, 768, WD[768], 1)
+        act_p(1, 1, 768, WD[768], 0)
+        mm_out(0, WD[0], 0)
+        mul_q(1, 512, WD[512], 1)
+        mm_out(0, WD[0], 3)
+        take_out(0, WD[0], 0, "S")
+        mul_q(1, 768, WD[768], 0)
+        take_out(0, WD[0], 3, "S")
+        mm_out(0, WD[0], 7)
+        quant_w(0, 512, WD[512])
+        add_w(1, 512, WD[512], 1)
+        mm_out(0, WD[0], 6)
+        take_out(0, WD[0], 7, "S")
+        mul_q(0, 768, WD[768], 0)
+        mm_out(0, WD[0], 2)
+        take_out(0, WD[0], 6, "S")
+        add_w(1, 512, WD[512], 0)
+        mm_out(0, WD[0], 4)
+        take_out(0, WD[0], 2, "S")
+        add_w(0, 768, WD[768], 0)
+        mm_out(0, WD[0], 1)
+        take_out(0, WD[0], 4, "S")
+        quant_w(1, 512, WD[512])
+        mm_out(0, WD[0], 5)
+        add_w(0, 768, WD[768], 1)
+        take_out(0, WD[0], 1, "S")
+        mm_out(512, WD[512], 0)
+        mul_q(1, 768, WD[768], 1)
+        take_out(0, WD[0], 5, "S")
+        mm_out(512, WD[512], 1)
+        take_out(512, WD[512], 0, "S")
+        quant_w(0, 768, WD[768])
+        add_w(1, 768, WD[768], 1)
+        mm_out(512, WD[512], 2)
+        take_out(512, WD[512], 1, "S")
+        add_w(1, 768, WD[768], 0)
+        mm_out(512, WD[512], 3)
+        take_out(512, WD[512], 2, "S")
+        quant_w(1, 768, WD[768])
+        take_out(512, WD[512], 3, "S")
+        mm_out(768, WD[768], 3)
+        mm_out(768, WD[768], 0)
+        take_out(768, WD[768], 3, "S")
+        mm_out(768, WD[768], 1)
+        take_out(768, WD[768], 0, "S")
+        mm_out(768, WD[768], 2)
+        take_out(768, WD[768], 1, "S")
+        take_out(768, WD[768], 2, "S")

@@ -15,7 +15,7 @@ FP8X4 = mybir.dt.float8_e4m3fn_x4
 ACT = mybir.ActivationFunctionType
 ALU = mybir.AluOpType
 
-WD = {0: 512, 512: 256, 768: 256}
+RANGES = [(0, 512), (512, 256), (768, 256)]
 
 
 def tile_fedparatanhhadamardlinear_kernel(
@@ -59,44 +59,46 @@ def tile_fedparatanhhadamardlinear_kernel(
             out=gain_bf[:].rearrange("p (g t) -> p g t", g=2),
             in_=gain.rearrange("(g p t) -> p g t", g=2, p=128, t=4),
         )
+        scale_kp = keep.tile([128, 8], F32, name="scale_kp")
+        nc.scalar.dma_start(
+            out=scale_kp[:], in_=x_scale.rearrange("o (m p) -> p (o m)", p=128)
+        )
         xs_t = keep.tile([128, 1024], F32, name="xs_t")
         y_raw = {}
         xr = {}
         w0_raw = {}
         xb = {}
 
-        def load_sc():
-            nc.sync.dma_start(
-                out=xs_t[:], in_=x_scale.rearrange("o k -> (o k)").partition_broadcast(128)
-            )
-
-        def load_y(w, h):
+        def load_y(w, r):
             y = y1 if w == 0 else y2
-            t = keep.tile([128, 4, 512], BF16, name="y%d%d" % (w, h))
+            f0, wd = RANGES[r]
+            t = keep.tile([128, 4, wd], BF16, name="y%d%d" % (w, r))
             nc.sync.dma_start(
-                out=t[:],
-                in_=y.rearrange("(p j) f -> p j f", j=4)[:, :, 512 * h : 512 * h + 512],
+                out=t[:], in_=y.rearrange("(p j) f -> p j f", j=4)[:, :, f0 : f0 + wd]
             )
-            y_raw[w, h] = t
+            y_raw[w, r] = t
 
-        def load_x12(w, g):
+        def load_x12(w, g, b=None):
             x = x1 if w == 0 else x2
-            t = keep.tile([128, 4, 512], BF16, name="x%d%d" % (w, g))
+            if (w, g) not in xr:
+                t = keep.tile([128, 4, 512], BF16, name="x%d%d" % (w, g))
+                xr[w, g] = t
+            ts = slice(0, 4) if b is None else slice(2 * b, 2 * b + 2)
             nc.sync.dma_start(
-                out=t[:],
-                in_=x.rearrange("(g m t) k -> g m t k", g=2, m=128, t=4)[g],
+                out=xr[w, g][:, ts, :],
+                in_=x.rearrange("(g m t) k -> g m t k", g=2, m=128, t=4)[g][:, ts, :],
             )
-            xr[w, g] = t
 
-        def load_w0(g, h):
-            t = keep.tile([128, 4, 512], BF16, name="w%d%d" % (g, h))
+        def load_w0(g, r):
+            f0, wd = RANGES[r]
+            t = keep.tile([128, 4, wd], BF16, name="w%d%d" % (g, r))
             nc.sync.dma_start(
                 out=t[:],
                 in_=w0.rearrange("(g m t) f -> g m t f", g=2, m=128, t=4)[
-                    g, :, :, 512 * h : 512 * h + 512
+                    g, :, :, f0 : f0 + wd
                 ],
             )
-            w0_raw[g, h] = t
+            w0_raw[g, r] = t
 
         def load_x(half):
             t = keep.tile([128, 4, 1024], U8, name="xb%d" % half)
@@ -107,10 +109,10 @@ def tile_fedparatanhhadamardlinear_kernel(
             xb[half] = t
 
         load_y(0, 0)
-        load_x12(0, 0)
+        load_x12(0, 0, 0)
+        load_x12(0, 0, 1)
         load_y(1, 0)
         load_x12(1, 0)
-        load_sc()
         load_x(0)
         load_x12(0, 1)
         load_x12(1, 1)
@@ -121,6 +123,10 @@ def tile_fedparatanhhadamardlinear_kernel(
         load_y(1, 1)
         load_w0(0, 1)
         load_w0(1, 1)
+        load_y(0, 2)
+        load_y(1, 2)
+        load_w0(0, 2)
+        load_w0(1, 2)
 
         x12c = keep.tile([128, 4, 512], U32, name="x12c", align_bytes=256)
         x12s = keep.tile([128, 4, 512], U8, name="x12s", align_bytes=256)
@@ -131,26 +137,40 @@ def tile_fedparatanhhadamardlinear_kernel(
         wc = keep.tile([128, 2, 1024], U32, name="wc", align_bytes=256)
         ws = keep.tile([128, 2, 1024], U8, name="ws", align_bytes=256)
 
+        banks = {}
         gain_f = keep.tile([128, 8], F32, name="gain_f")
         gain_1 = keep.tile([128, 8], F32, name="gain_1")
         diag = keep.tile([128, 8, 128], BF16, name="diag")
 
-        def prep_gain():
-            nc.vector.tensor_copy(out=gain_f[:], in_=gain_bf[:])
-            nc.vector.tensor_scalar(
-                out=gain_1[:], in0=gain_bf[:], scalar1=0.1, scalar2=None, op0=ALU.mult
+        nc.gpsimd.tensor_copy(out=gain_f[:], in_=gain_bf[:])
+        nc.gpsimd.tensor_scalar(
+            out=gain_1[:], in0=gain_bf[:], scalar1=0.1, scalar2=0.0, op0=ALU.mult, op1=ALU.add
+        )
+        for j in range(8):
+            nc.gpsimd.tensor_scalar(
+                out=diag[:, j, :],
+                in0=identb[:],
+                scalar1=gain_f[:, j : j + 1],
+                scalar2=0.0,
+                op0=ALU.mult,
+                op1=ALU.add,
             )
-            for j in range(8):
-                nc.vector.tensor_scalar(
-                    out=diag[:, j, :],
-                    in0=identb[:],
-                    scalar1=gain_f[:, j : j + 1],
-                    scalar2=None,
-                    op0=ALU.mult,
+
+        def turn_scale(b):
+            pb = bank()
+            for a in range(4):
+                m = 4 * b + a
+                nc.tensor.transpose(
+                    pb[:, 128 * a : 128 * a + 128],
+                    scale_kp[:, m : m + 1].to_broadcast([128, 128]),
+                    ident[:],
                 )
+            banks["sc", b] = pb
+
+        def take_scale(b, eng):
+            take(eng, xs_t[:, 512 * b : 512 * b + 512], banks["sc", b][:])
 
         xt12 = {}
-        banks = {}
 
         def turn_x12(w, g, b):
             words = xr[w, g][:].rearrange("p t k -> p (t k)").bitcast(F32)
@@ -177,51 +197,59 @@ def tile_fedparatanhhadamardlinear_kernel(
                 banks["x12", w, g, b][:].rearrange("p (t u m) -> p t m u", t=2, u=2),
             )
 
-        def quant_x12(w, g):
+        def quant_x12(w, g, b=None):
+            c = slice(0, 512) if b is None else slice(256 * b, 256 * b + 256)
+            i = slice(0, 2048) if b is None else slice(1024 * b, 1024 * b + 1024)
             nc.vector.quantize_mx(
-                out=x12c[:, 2 * w + g, :].bitcast(FP8X4),
-                scales=x12s[:, 2 * w + g, :],
-                in_=xt12[w, g][:],
+                out=x12c[:, 2 * w + g, c].bitcast(FP8X4),
+                scales=x12s[:, 2 * w + g, c],
+                in_=xt12[w, g][:, i],
             )
 
         yg = {}
 
-        def new_yg(w, h):
-            if (w, h) not in yg:
-                t = work.tile([128, 512, 4], BF16, name="yg", tag="yg", bufs=3, align_bytes=256)
-                yg[w, h] = t
-            return yg[w, h]
+        def new_yg(w, r):
+            if (w, r) not in yg:
+                t = work.tile(
+                    [128, RANGES[r][1], 4], BF16, name="yg", tag="yg", bufs=3, align_bytes=256
+                )
+                yg[w, r] = t
+            return yg[w, r]
 
-        def lay_y(w, h):
-            t = new_yg(w, h)
-            nc.vector.tensor_copy(out=t[:], in_=y_raw[w, h][:].rearrange("p j f -> p f j"))
+        def lay_y(w, r, eng):
+            take(
+                eng,
+                new_yg(w, r)[:].rearrange("p (c i) j -> p c j i", i=4),
+                y_raw[w, r][:].rearrange("p j (c i) -> p c j i", i=4),
+            )
 
-        def turn_y(w, h, b):
+        def turn_y(w, r, b):
             pb = psum.tile([128, 1024], BF16, name="bank", tag="bank")
             for a in range(2):
                 n = 256 * b + 128 * a
                 nc.tensor.matmul(
                     pb[:, 512 * a : 512 * a + 512],
                     lhsT=identb[:],
-                    rhs=y_raw[w, h][:, :, n : n + 128].rearrange("p j n -> p n j"),
+                    rhs=y_raw[w, r][:, :, n : n + 128].rearrange("p j n -> p n j"),
                     start=True,
                     stop=True,
                 )
-            banks["y", w, h, b] = pb
+            banks["y", w, r, b] = pb
 
-        def take_y(w, h, b, eng):
-            t = new_yg(w, h)
+        def take_y(w, r, b, eng):
+            t = new_yg(w, r)
             take(
                 eng,
                 t[:].rearrange("p f j -> p (f j)").bitcast(F32)[:, 512 * b : 512 * b + 512],
-                banks["y", w, h, b][:].bitcast(F32),
+                banks["y", w, r, b][:].bitcast(F32),
             )
 
-        def quant_y(w, h):
+        def quant_y(w, r):
+            f0, wd = RANGES[r]
             nc.vector.quantize_mx(
-                out=yc[:, w, 512 * h : 512 * h + 512].bitcast(FP8X4),
-                scales=ys[:, w, 512 * h : 512 * h + 512],
-                in_=yg[w, h][:].rearrange("p f j -> p (f j)"),
+                out=yc[:, w, f0 : f0 + wd].bitcast(FP8X4),
+                scales=ys[:, w, f0 : f0 + wd],
+                in_=yg[w, r][:].rearrange("p f j -> p (f j)"),
             )
 
         xw = {}
@@ -268,7 +296,8 @@ def tile_fedparatanhhadamardlinear_kernel(
 
         pt = {}
 
-        def mm_p(w, g, f0, wd, j):
+        def mm_p(w, g, r, j):
+            f0, wd = RANGES[r]
             per = 512 // wd
             pb = bank()
             for a in range(per):
@@ -284,7 +313,8 @@ def tile_fedparatanhhadamardlinear_kernel(
                 )
             banks["p", w, g, f0, j] = pb
 
-        def act_p(w, g, f0, wd, j):
+        def act_p(w, g, r, j):
+            f0, wd = RANGES[r]
             pb = banks["p", w, g, f0, j]
             if w == 0:
                 a = work.tile([128, 512], F32, name="t1", tag="t1", bufs=6)
@@ -297,7 +327,8 @@ def tile_fedparatanhhadamardlinear_kernel(
         qt = {}
         wb = {}
 
-        def mul_q(g, f0, wd, j):
+        def mul_q(g, r, j):
+            f0, wd = RANGES[r]
             per = 512 // wd
             if (g, f0) not in qt:
                 q = work.tile([128, 4, wd], F32, name="qt", tag="qt", bufs=3)
@@ -314,38 +345,41 @@ def tile_fedparatanhhadamardlinear_kernel(
                     op1=ALU.mult,
                 )
 
-        def mm_g(g, f0, wd, n):
+        def mm_g(g, r, n):
             pb = bank()
-            o = f0 % 512 + 128 * n
+            o = 128 * n
             for t in range(4):
                 nc.tensor.matmul(
                     pb[:, 128 * t : 128 * t + 128],
                     lhsT=diag[:, 4 * g + t, :],
-                    rhs=w0_raw[g, f0 // 512][:, t, o : o + 128],
+                    rhs=w0_raw[g, r][:, t, o : o + 128],
                     start=True,
                     stop=True,
                 )
-            banks["g", g, f0, n] = pb
+            banks["g", g, r, n] = pb
 
-        def add_w(g, f0, wd, n):
+        def add_w(g, r, n):
+            f0, wd = RANGES[r]
             if (g, f0) not in wb:
                 t = work.tile([128, 4 * wd], BF16, name="wb", tag="wb", bufs=3, align_bytes=256)
                 wb[g, f0] = t
             nc.vector.tensor_tensor(
                 out=wb[g, f0][:, 512 * n : 512 * n + 512].rearrange("p (n t) -> p n t", t=4),
-                in0=banks["g", g, f0, n][:].rearrange("p (t n) -> p n t", t=4),
+                in0=banks["g", g, r, n][:].rearrange("p (t n) -> p n t", t=4),
                 in1=qt[g, f0][:, :, 128 * n : 128 * n + 128].rearrange("p t n -> p n t"),
                 op=ALU.add,
             )
 
-        def quant_w(g, f0, wd):
+        def quant_w(g, r):
+            f0, wd = RANGES[r]
             nc.vector.quantize_mx(
                 out=wc[:, g, f0 : f0 + wd].bitcast(FP8X4),
                 scales=ws[:, g, f0 : f0 + wd],
                 in_=wb[g, f0][:],
             )
 
-        def mm_out(f0, wd, k):
+        def mm_out(r, k):
+            f0, wd = RANGES[r]
             per = 512 // wd
             pb = bank()
             for a in range(per):
@@ -362,7 +396,8 @@ def tile_fedparatanhhadamardlinear_kernel(
                     )
             banks["o", f0, k] = pb
 
-        def take_out(f0, wd, k, eng):
+        def take_out(r, k, eng):
+            f0, wd = RANGES[r]
             per = 512 // wd
             o = work.tile([128, per, wd], F32, name="o", tag="o", bufs=6)
             take(eng, o[:].rearrange("p a f -> p (a f)"), banks["o", f0, k][:])
@@ -371,217 +406,218 @@ def tile_fedparatanhhadamardlinear_kernel(
                 in_=o[:],
             )
 
-        pass
-        lay_y(0, 0)
-        turn_x12(0, 0, 1)
+        lay_y(0, 0, "V")
         turn_x12(0, 0, 0)
-        quant_y(0, 0)
-        take_x12(0, 0, 1, "S")
-        lay_y(1, 0)
+        turn_scale(1)
         take_x12(0, 0, 0, "S")
+        quant_y(0, 0)
+        turn_x12(0, 0, 1)
+        take_scale(1, "S")
+        quant_x12(0, 0, 0)
+        turn_scale(0)
+        take_x12(0, 0, 1, "S")
+        lay_y(1, 0, "V")
+        mm_p(0, 0, 0, 1)
+        take_scale(0, "S")
+        mm_p(0, 0, 0, 0)
+        act_p(0, 0, 0, 1)
         turn_x12(1, 0, 1)
-        quant_x12(0, 0)
+        quant_x12(0, 0, 1)
+        act_p(0, 0, 0, 0)
+        quant_y(1, 0)
         turn_x12(1, 0, 0)
         take_x12(1, 0, 1, "S")
-        quant_y(1, 0)
-        mm_p(0, 0, 0, WD[0], 2)
-        take_x12(1, 0, 0, "S")
-        mm_p(0, 0, 0, WD[0], 0)
-        act_p(0, 0, 0, WD[0], 2)
-        mm_p(0, 0, 0, WD[0], 3)
-        quant_x12(1, 0)
-        prep_gain()
-        mm_p(0, 0, 0, WD[0], 1)
-        act_p(0, 0, 0, WD[0], 3)
-        scale_x(1)
-        mm_p(1, 0, 0, WD[0], 1)
-        act_p(0, 0, 0, WD[0], 0)
-        mm_p(1, 0, 0, WD[0], 0)
-        turn_x12(0, 1, 1)
-        act_p(1, 0, 0, WD[0], 1)
-        scale_x(3)
-        turn_x(1)
-        act_p(1, 0, 0, WD[0], 0)
-        mm_p(1, 0, 0, WD[0], 2)
-        act_p(0, 0, 0, WD[0], 1)
-        mul_q(0, 0, WD[0], 0)
-        turn_x12(1, 1, 0)
-        act_p(1, 0, 0, WD[0], 2)
+        mm_p(0, 0, 0, 2)
         scale_x(0)
-        mm_g(0, 0, WD[0], 2)
-        take_x(1, "S")
-        mm_p(1, 0, 0, WD[0], 3)
+        take_x12(1, 0, 0, "S")
+        mm_p(0, 0, 0, 3)
+        act_p(0, 0, 0, 2)
+        quant_x12(1, 0)
         turn_x12(0, 1, 0)
-        take_x12(0, 1, 1, "S")
-        mul_q(0, 0, WD[0], 1)
-        act_p(1, 0, 0, WD[0], 3)
-        mm_g(1, 0, WD[0], 0)
-        mul_q(0, 0, WD[0], 2)
-        mm_g(1, 0, WD[0], 1)
+        act_p(0, 0, 0, 3)
+        scale_x(1)
+        turn_x12(0, 1, 1)
         take_x12(0, 1, 0, "S")
-        scale_x(6)
-        turn_x12(1, 1, 1)
-        take_x12(1, 1, 0, "S")
-        turn_x(0)
-        take_x12(1, 1, 1, "S")
-        quant_x12(0, 1)
-        turn_y(0, 1, 1)
-        take_x(0, "S")
-        scale_x(5)
-        turn_y(0, 1, 0)
-        take_y(0, 1, 1, "S")
-        mm_p(0, 1, 0, WD[0], 3)
-        quant_x12(1, 1)
-        take_y(0, 1, 0, "S")
-        turn_y(1, 1, 1)
-        act_p(0, 1, 0, WD[0], 3)
-        scale_x(4)
-        mm_g(0, 512, WD[512], 0)
-        mm_p(1, 1, 0, WD[0], 2)
-        take_y(1, 1, 1, "S")
-        mm_p(1, 1, 0, WD[0], 1)
-        mm_p(1, 1, 0, WD[0], 3)
-        act_p(1, 1, 0, WD[0], 2)
-        quant_y(0, 1)
-        mm_p(1, 1, 0, WD[0], 0)
-        act_p(1, 1, 0, WD[0], 3)
-        mul_q(0, 0, WD[0], 3)
-        turn_x(4)
-        act_p(1, 1, 0, WD[0], 1)
+        mm_p(1, 0, 0, 0)
+        take_x12(0, 1, 1, "S")
+        mm_p(1, 0, 0, 1)
         scale_x(2)
-        mm_p(0, 1, 512, WD[512], 1)
-        take_x(4, "S")
-        mm_g(1, 0, WD[0], 2)
-        act_p(1, 1, 0, WD[0], 0)
-        add_w(0, 0, WD[0], 2)
-        mm_p(0, 1, 0, WD[0], 1)
-        act_p(0, 1, 512, WD[512], 1)
-        mul_q(1, 0, WD[0], 3)
+        turn_x(1)
+        act_p(1, 0, 0, 0)
+        mm_p(1, 0, 0, 2)
+        act_p(1, 0, 0, 1)
+        quant_x12(0, 1)
+        turn_x12(1, 1, 1)
+        take_x(1, "S")
+        mul_q(0, 0, 0)
+        turn_x12(1, 1, 0)
+        act_p(1, 0, 0, 2)
+        take_x12(1, 1, 1, "V")
+        mm_p(1, 0, 0, 3)
+        take_x12(1, 1, 0, "S")
+        mul_q(0, 0, 1)
+        turn_x(0)
+        act_p(1, 0, 0, 3)
+        mul_q(0, 0, 2)
+        mm_p(0, 1, 0, 0)
+        take_x(0, "S")
+        mm_p(0, 1, 0, 1)
+        quant_x12(1, 1)
+        mm_g(0, 0, 1)
+        act_p(0, 1, 0, 0)
+        mul_q(0, 0, 3)
+        mm_g(0, 0, 2)
+        mm_p(1, 1, 0, 1)
+        act_p(0, 1, 0, 1)
+        scale_x(3)
+        mm_p(1, 1, 0, 0)
+        mm_g(0, 0, 0)
+        act_p(1, 1, 0, 1)
         turn_x(2)
-        act_p(0, 1, 0, WD[0], 1)
-        scale_x(7)
-        mm_g(0, 0, WD[0], 1)
-        take_x(2, "S")
-        mm_p(0, 1, 0, WD[0], 0)
-        mm_p(0, 1, 0, WD[0], 2)
-        add_w(0, 0, WD[0], 1)
-        act_p(0, 1, 0, WD[0], 0)
-        mm_g(0, 0, WD[0], 3)
-        mul_q(1, 0, WD[0], 1)
-        act_p(0, 1, 0, WD[0], 2)
-        turn_x(7)
-        mul_q(1, 0, WD[0], 0)
-        turn_y(1, 1, 0)
-        take_x(7, "S")
-        mul_q(1, 0, WD[0], 2)
+        act_p(1, 1, 0, 0)
+        add_w(0, 0, 1)
         turn_x(3)
-        take_y(1, 1, 0, "S")
-        add_w(0, 0, WD[0], 3)
-        turn_x(6)
-        add_w(1, 0, WD[0], 0)
-        take_x(3, "S")
-        mm_g(0, 0, WD[0], 0)
+        take_x(2, "S")
+        add_w(0, 0, 0)
+        mm_g(0, 0, 3)
+        lay_y(1, 1, "S")
+        mm_p(0, 1, 0, 2)
+        mul_q(1, 0, 1)
+        mm_p(1, 1, 0, 2)
+        mm_p(1, 1, 0, 3)
+        add_w(0, 0, 3)
+        mm_p(0, 1, 0, 3)
+        act_p(1, 1, 0, 2)
+        mm_g(1, 0, 0)
+        add_w(0, 0, 2)
+        mm_g(1, 0, 1)
+        lay_y(0, 1, "S")
+        mm_g(1, 1, 1)
         quant_y(1, 1)
-        take_x(6, "S")
-        mm_p(0, 0, 512, WD[512], 1)
-        mm_p(0, 0, 512, WD[512], 0)
+        mm_g(0, 1, 1)
+        quant_w(0, 0)
+        act_p(0, 1, 0, 2)
+        scale_x(4)
+        act_p(1, 1, 0, 3)
+        mm_p(1, 0, 1, 0)
+        quant_y(0, 1)
+        take_x(3, "S")
+        mm_p(1, 0, 1, 1)
+        mul_q(1, 0, 2)
+        act_p(0, 1, 0, 3)
+        turn_x(4)
         quant_x(0, 0)
-        act_p(0, 0, 512, WD[512], 1)
-        mm_p(1, 1, 512, WD[512], 1)
-        mm_p(1, 0, 768, WD[768], 0)
-        add_w(0, 0, WD[0], 0)
-        act_p(1, 1, 512, WD[512], 1)
-        mm_p(1, 0, 512, WD[512], 0)
+        act_p(1, 0, 1, 1)
+        mm_p(0, 0, 1, 0)
         quant_x(0, 1)
-        mm_p(1, 0, 768, WD[768], 1)
-        act_p(1, 0, 768, WD[768], 0)
-        mm_g(1, 0, WD[0], 3)
-        add_w(1, 0, WD[0], 1)
-        act_p(0, 0, 512, WD[512], 0)
-        mm_g(1, 512, WD[512], 1)
-        add_w(1, 0, WD[0], 3)
+        take_x(4, "S")
+        mm_p(0, 1, 1, 0)
+        scale_x(6)
+        act_p(0, 0, 1, 0)
+        mm_g(1, 0, 3)
+        act_p(0, 1, 1, 0)
+        mm_p(1, 1, 1, 0)
+        mul_q(1, 0, 0)
+        act_p(1, 0, 1, 0)
+        turn_x(6)
+        scale_x(7)
+        act_p(1, 1, 1, 0)
+        mm_p(0, 0, 1, 1)
+        take_x(6, "S")
+        mm_g(0, 1, 0)
+        mul_q(0, 1, 0)
+        lay_y(1, 2, "S")
+        turn_x(7)
+        scale_x(5)
+        take_x(7, "S")
+        mul_q(1, 0, 3)
+        lay_y(0, 2, "S")
         turn_x(5)
-        act_p(1, 0, 512, WD[512], 0)
-        add_w(1, 0, WD[0], 2)
-        act_p(1, 0, 768, WD[768], 1)
-        mm_g(0, 512, WD[512], 1)
-        mul_q(0, 512, WD[512], 0)
-        mm_p(1, 0, 512, WD[512], 1)
+        quant_y(1, 2)
+        add_w(1, 0, 1)
+        add_w(1, 0, 3)
+        mm_p(1, 1, 1, 1)
         take_x(5, "S")
-        mm_p(0, 1, 768, WD[768], 0)
-        quant_w(0, 0, WD[0])
-        mm_p(0, 1, 512, WD[512], 0)
-        act_p(1, 0, 512, WD[512], 1)
-        mm_p(0, 0, 768, WD[768], 0)
-        quant_x(1, 0)
-        mm_p(0, 1, 768, WD[768], 1)
-        act_p(0, 1, 512, WD[512], 0)
-        mm_g(1, 768, WD[768], 1)
-        mul_q(0, 512, WD[512], 1)
-        act_p(0, 1, 768, WD[768], 1)
-        mm_g(1, 768, WD[768], 0)
+        quant_y(0, 2)
+        act_p(0, 0, 1, 1)
+        mm_p(1, 0, 2, 0)
+        add_w(1, 0, 0)
+        mm_p(0, 1, 1, 1)
+        act_p(1, 1, 1, 1)
+        mm_p(0, 0, 2, 1)
+        mul_q(0, 1, 1)
+        mm_g(1, 1, 0)
+        act_p(0, 1, 1, 1)
+        mm_g(1, 0, 2)
         quant_x(1, 1)
-        act_p(0, 0, 768, WD[768], 0)
-        mm_p(1, 1, 512, WD[512], 0)
-        add_w(0, 512, WD[512], 0)
-        act_p(0, 1, 768, WD[768], 0)
-        mm_g(0, 768, WD[768], 1)
-        add_w(0, 512, WD[512], 1)
-        act_p(1, 1, 512, WD[512], 0)
-        mm_p(0, 0, 768, WD[768], 1)
-        mm_p(1, 1, 768, WD[768], 1)
-        quant_w(1, 0, WD[0])
-        act_p(0, 0, 768, WD[768], 1)
-        mm_p(1, 1, 768, WD[768], 0)
-        mm_g(1, 512, WD[512], 0)
-        mul_q(1, 512, WD[512], 0)
-        act_p(1, 1, 768, WD[768], 1)
-        mm_g(0, 768, WD[768], 0)
-        mul_q(0, 768, WD[768], 1)
-        act_p(1, 1, 768, WD[768], 0)
-        mm_out(0, WD[0], 0)
-        mul_q(1, 512, WD[512], 1)
-        mm_out(0, WD[0], 3)
-        take_out(0, WD[0], 0, "S")
-        mul_q(1, 768, WD[768], 0)
-        take_out(0, WD[0], 3, "S")
-        mm_out(0, WD[0], 7)
-        quant_w(0, 512, WD[512])
-        add_w(1, 512, WD[512], 1)
-        mm_out(0, WD[0], 6)
-        take_out(0, WD[0], 7, "S")
-        mul_q(0, 768, WD[768], 0)
-        mm_out(0, WD[0], 2)
-        take_out(0, WD[0], 6, "S")
-        add_w(1, 512, WD[512], 0)
-        mm_out(0, WD[0], 4)
-        take_out(0, WD[0], 2, "S")
-        add_w(0, 768, WD[768], 0)
-        mm_out(0, WD[0], 1)
-        take_out(0, WD[0], 4, "S")
-        quant_w(1, 512, WD[512])
-        mm_out(0, WD[0], 5)
-        add_w(0, 768, WD[768], 1)
-        take_out(0, WD[0], 1, "S")
-        mm_out(512, WD[512], 0)
-        mul_q(1, 768, WD[768], 1)
-        take_out(0, WD[0], 5, "S")
-        mm_out(512, WD[512], 1)
-        take_out(512, WD[512], 0, "S")
-        quant_w(0, 768, WD[768])
-        add_w(1, 768, WD[768], 1)
-        mm_out(512, WD[512], 2)
-        take_out(512, WD[512], 1, "S")
-        add_w(1, 768, WD[768], 0)
-        mm_out(512, WD[512], 3)
-        take_out(512, WD[512], 2, "S")
-        quant_w(1, 768, WD[768])
-        take_out(512, WD[512], 3, "S")
-        mm_out(768, WD[768], 3)
-        mm_out(768, WD[768], 0)
-        take_out(768, WD[768], 3, "S")
-        mm_out(768, WD[768], 1)
-        take_out(768, WD[768], 0, "S")
-        mm_out(768, WD[768], 2)
-        take_out(768, WD[768], 1, "S")
-        take_out(768, WD[768], 2, "S")
+        act_p(0, 0, 2, 1)
+        mm_p(1, 0, 2, 1)
+        add_w(1, 0, 2)
+        act_p(1, 0, 2, 0)
+        mm_p(1, 1, 2, 0)
+        add_w(0, 1, 0)
+        act_p(1, 0, 2, 1)
+        mm_p(0, 1, 2, 0)
+        mm_g(1, 2, 0)
+        act_p(0, 1, 2, 0)
+        quant_w(1, 0)
+        mm_p(0, 0, 2, 0)
+        mm_g(0, 2, 0)
+        act_p(1, 1, 2, 0)
+        quant_x(1, 0)
+        mm_out(0, 0)
+        act_p(0, 0, 2, 0)
+        add_w(0, 1, 1)
+        mm_out(0, 1)
+        take_out(0, 0, "S")
+        mul_q(1, 1, 0)
+        mm_out(0, 4)
+        take_out(0, 1, "S")
+        quant_w(0, 1)
+        mm_out(0, 2)
+        take_out(0, 4, "S")
+        mul_q(1, 1, 1)
+        mm_out(0, 3)
+        take_out(0, 2, "S")
+        mul_q(0, 2, 0)
+        mm_out(0, 5)
+        take_out(0, 3, "S")
+        add_w(1, 1, 0)
+        mm_out(0, 7)
+        take_out(0, 5, "S")
+        add_w(1, 1, 1)
+        mm_p(0, 1, 2, 1)
+        take_out(0, 7, "S")
+        mm_g(1, 2, 1)
+        mm_g(0, 2, 1)
+        mul_q(0, 2, 1)
+        act_p(0, 1, 2, 1)
+        mm_p(1, 1, 2, 1)
+        quant_w(1, 1)
+        mm_out(0, 6)
+        act_p(1, 1, 2, 1)
+        add_w(0, 2, 1)
+        mm_out(1, 1)
+        take_out(0, 6, "S")
+        mul_q(1, 2, 0)
+        mm_out(1, 0)
+        take_out(1, 1, "S")
+        add_w(0, 2, 0)
+        mm_out(1, 2)
+        take_out(1, 0, "S")
+        mul_q(1, 2, 1)
+        mm_out(1, 3)
+        take_out(1, 2, "S")
+        quant_w(0, 2)
+        take_out(1, 3, "S")
+        add_w(1, 2, 0)
+        add_w(1, 2, 1)
+        quant_w(1, 2)
+        mm_out(2, 0)
+        mm_out(2, 1)
+        take_out(2, 0, "S")
+        mm_out(2, 2)
+        take_out(2, 1, "S")
+        mm_out(2, 3)
+        take_out(2, 2, "S")
+        take_out(2, 3, "S")

@@ -15,7 +15,8 @@ FP8X4 = mybir.dt.float8_e4m3fn_x4
 ACT = mybir.ActivationFunctionType
 ALU = mybir.AluOpType
 
-RANGES = [(0, 512), (512, 256), (768, 256)]
+YPARTS = [(0, 512), (512, 256), (768, 256)]
+RANGES = [(0, 512), (512, 256), (768, 128), (896, 128)]
 
 
 def tile_fedparatanhhadamardlinear_kernel(
@@ -46,14 +47,6 @@ def tile_fedparatanhhadamardlinear_kernel(
             else:
                 nc.vector.tensor_copy(out=dst, in_=src)
 
-        warm = keep.tile([128, 1], F32, name="warm")
-        nc.vector.memset(warm[:], 0.0)
-        nc.scalar.activation(warm[:], warm[:], ACT.Sigmoid)
-        ident = keep.tile([128, 128], F32, name="ident")
-        make_identity(nc, ident[:])
-        identb = keep.tile([128, 128], BF16, name="identb")
-        make_identity(nc, identb[:])
-
         gain_bf = keep.tile([128, 8], BF16, name="gain_bf")
         nc.scalar.dma_start(
             out=gain_bf[:].rearrange("p (g t) -> p g t", g=2),
@@ -63,6 +56,19 @@ def tile_fedparatanhhadamardlinear_kernel(
         nc.scalar.dma_start(
             out=scale_kp[:], in_=x_scale.rearrange("o (m p) -> p (o m)", p=128)
         )
+        warm = keep.tile([128, 1], F32, name="warm")
+        nc.vector.memset(warm[:], 0.0)
+        nc.scalar.activation(warm[:], warm[:], ACT.Sigmoid)
+        ident = keep.tile([128, 128], F32, name="ident")
+        make_identity(nc, ident[:])
+        identb = keep.tile([128, 128], BF16, name="identb")
+        make_identity(nc, identb[:])
+
+        zeros = keep.tile([128, 512], BF16, name="zeros")
+        nc.vector.memset(zeros[:], 0.0)
+        idle = bank()
+        for n in range(6):
+            nc.tensor.matmul(idle[:], lhsT=zeros[:, 0:128], rhs=zeros[:], start=True, stop=True)
         xs_t = keep.tile([128, 1024], F32, name="xs_t")
         y_raw = {}
         xr = {}
@@ -71,7 +77,7 @@ def tile_fedparatanhhadamardlinear_kernel(
 
         def load_y(w, r):
             y = y1 if w == 0 else y2
-            f0, wd = RANGES[r]
+            f0, wd = 512 * r, 512
             t = keep.tile([128, 4, wd], BF16, name="y%d%d" % (w, r))
             nc.sync.dma_start(
                 out=t[:], in_=y.rearrange("(p j) f -> p j f", j=4)[:, :, f0 : f0 + wd]
@@ -90,7 +96,7 @@ def tile_fedparatanhhadamardlinear_kernel(
             )
 
         def load_w0(g, r):
-            f0, wd = RANGES[r]
+            f0, wd = 512 * r, 512
             t = keep.tile([128, 4, wd], BF16, name="w%d%d" % (g, r))
             nc.sync.dma_start(
                 out=t[:],
@@ -108,6 +114,7 @@ def tile_fedparatanhhadamardlinear_kernel(
             )
             xb[half] = t
 
+
         load_y(0, 0)
         load_x12(0, 0, 0)
         load_x12(0, 0, 1)
@@ -123,17 +130,13 @@ def tile_fedparatanhhadamardlinear_kernel(
         load_y(1, 1)
         load_w0(0, 1)
         load_w0(1, 1)
-        load_y(0, 2)
-        load_y(1, 2)
-        load_w0(0, 2)
-        load_w0(1, 2)
 
         x12c = keep.tile([128, 4, 512], U32, name="x12c", align_bytes=256)
         x12s = keep.tile([128, 4, 512], U8, name="x12s", align_bytes=256)
         yc = keep.tile([128, 2, 1024], U32, name="yc", align_bytes=256)
         ys = keep.tile([128, 2, 1024], U8, name="ys", align_bytes=256)
-        xc = keep.tile([128, 2, 1024], U32, name="xc", align_bytes=256)
-        xsc = keep.tile([128, 2, 1024], U8, name="xsc", align_bytes=256)
+        xc = keep.tile([128, 2, 2, 512], U32, name="xc", align_bytes=256)
+        xsc = keep.tile([128, 2, 2, 512], U8, name="xsc", align_bytes=256)
         wc = keep.tile([128, 2, 1024], U32, name="wc", align_bytes=256)
         ws = keep.tile([128, 2, 1024], U8, name="ws", align_bytes=256)
 
@@ -142,19 +145,13 @@ def tile_fedparatanhhadamardlinear_kernel(
         gain_1 = keep.tile([128, 8], F32, name="gain_1")
         diag = keep.tile([128, 8, 128], BF16, name="diag")
 
-        nc.gpsimd.tensor_copy(out=gain_f[:], in_=gain_bf[:])
-        nc.gpsimd.tensor_scalar(
-            out=gain_1[:], in0=gain_bf[:], scalar1=0.1, scalar2=0.0, op0=ALU.mult, op1=ALU.add
-        )
-        for j in range(8):
-            nc.gpsimd.tensor_scalar(
-                out=diag[:, j, :],
-                in0=identb[:],
-                scalar1=gain_f[:, j : j + 1],
-                scalar2=0.0,
-                op0=ALU.mult,
-                op1=ALU.add,
-            )
+        def prep_gain():
+            nc.scalar.copy(gain_f[:], gain_bf[:])
+            nc.scalar.activation(gain_1[:], gain_bf[:], ACT.Copy, scale=0.1)
+            for j in range(8):
+                nc.scalar.activation(
+                    diag[:, j, :], identb[:], ACT.Copy, scale=gain_f[:, j : j + 1]
+                )
 
         def turn_scale(b):
             pb = bank()
@@ -187,7 +184,7 @@ def tile_fedparatanhhadamardlinear_kernel(
 
         def take_x12(w, g, b, eng):
             if (w, g) not in xt12:
-                t = work.tile([128, 2048], BF16, name="xt12", tag="xt12", bufs=4, align_bytes=256)
+                t = work.tile([128, 2048], BF16, name="xt12", tag="xt12", bufs=3, align_bytes=256)
                 xt12[w, g] = t
             take(
                 eng,
@@ -211,7 +208,7 @@ def tile_fedparatanhhadamardlinear_kernel(
         def new_yg(w, r):
             if (w, r) not in yg:
                 t = work.tile(
-                    [128, RANGES[r][1], 4], BF16, name="yg", tag="yg", bufs=3, align_bytes=256
+                    [128, YPARTS[r][1], 4], BF16, name="yg", tag="yg", bufs=3, align_bytes=256
                 )
                 yg[w, r] = t
             return yg[w, r]
@@ -220,17 +217,19 @@ def tile_fedparatanhhadamardlinear_kernel(
             take(
                 eng,
                 new_yg(w, r)[:].rearrange("p (c i) j -> p c j i", i=4),
-                y_raw[w, r][:].rearrange("p j (c i) -> p c j i", i=4),
+                y_raw[w, YPARTS[r][0] // 512][
+                    :, :, YPARTS[r][0] % 512 : YPARTS[r][0] % 512 + YPARTS[r][1]
+                ].rearrange("p j (c i) -> p c j i", i=4),
             )
 
         def turn_y(w, r, b):
             pb = psum.tile([128, 1024], BF16, name="bank", tag="bank")
             for a in range(2):
-                n = 256 * b + 128 * a
+                n = YPARTS[r][0] % 512 + 256 * b + 128 * a
                 nc.tensor.matmul(
                     pb[:, 512 * a : 512 * a + 512],
                     lhsT=identb[:],
-                    rhs=y_raw[w, r][:, :, n : n + 128].rearrange("p j n -> p n j"),
+                    rhs=y_raw[w, YPARTS[r][0] // 512][:, :, n : n + 128].rearrange("p j n -> p n j"),
                     start=True,
                     stop=True,
                 )
@@ -245,7 +244,7 @@ def tile_fedparatanhhadamardlinear_kernel(
             )
 
         def quant_y(w, r):
-            f0, wd = RANGES[r]
+            f0, wd = YPARTS[r]
             nc.vector.quantize_mx(
                 out=yc[:, w, f0 : f0 + wd].bitcast(FP8X4),
                 scales=ys[:, w, f0 : f0 + wd],
@@ -256,7 +255,7 @@ def tile_fedparatanhhadamardlinear_kernel(
         xt = {}
 
         def scale_x(i):
-            t = work.tile([128, 1024], BF16, name="xw", tag="xw", bufs=4, align_bytes=256)
+            t = work.tile([128, 1024], BF16, name="xw", tag="xw", bufs=8, align_bytes=256)
             nc.vector.tensor_tensor(
                 out=t[:], in0=xb[i // 4][:, i % 4, :].bitcast(FP8), in1=xs_t[:], op=ALU.mult
             )
@@ -287,11 +286,11 @@ def tile_fedparatanhhadamardlinear_kernel(
                 banks["x", i][:].rearrange("p (g u r) -> p g r u", g=2, u=2),
             )
 
-        def quant_x(half, g):
+        def quant_x(half):
             nc.vector.quantize_mx(
-                out=xc[:, g, 512 * half : 512 * half + 512].bitcast(FP8X4),
-                scales=xsc[:, g, 512 * half : 512 * half + 512],
-                in_=xt[half][:, g, :],
+                out=xc[:, half, :, :].rearrange("p g r -> p (g r)").bitcast(FP8X4),
+                scales=xsc[:, half, :, :].rearrange("p g r -> p (g r)"),
+                in_=xt[half][:].rearrange("p g c -> p (g c)"),
             )
 
         pt = {}
@@ -347,12 +346,12 @@ def tile_fedparatanhhadamardlinear_kernel(
 
         def mm_g(g, r, n):
             pb = bank()
-            o = 128 * n
+            o = RANGES[r][0] % 512 + 128 * n
             for t in range(4):
                 nc.tensor.matmul(
                     pb[:, 128 * t : 128 * t + 128],
                     lhsT=diag[:, 4 * g + t, :],
-                    rhs=w0_raw[g, r][:, t, o : o + 128],
+                    rhs=w0_raw[g, RANGES[r][0] // 512][:, t, o : o + 128],
                     start=True,
                     stop=True,
                 )
@@ -387,8 +386,8 @@ def tile_fedparatanhhadamardlinear_kernel(
                 for g in range(2):
                     nc.tensor.matmul_mx(
                         out=pb[:, a * wd : (a + 1) * wd],
-                        lhsT=xc[:, g, 128 * i : 128 * i + 128].bitcast(FP8X4),
-                        lhsT_scale=xsc[:, g, 128 * i : 128 * i + 128],
+                        lhsT=xc[:, i // 4, g, 128 * (i % 4) : 128 * (i % 4) + 128].bitcast(FP8X4),
+                        lhsT_scale=xsc[:, i // 4, g, 128 * (i % 4) : 128 * (i % 4) + 128],
                         rhs=wc[:, g, f0 : f0 + wd].bitcast(FP8X4),
                         rhs_scale=ws[:, g, f0 : f0 + wd],
                         start=(g == 0),
@@ -399,225 +398,226 @@ def tile_fedparatanhhadamardlinear_kernel(
         def take_out(r, k, eng):
             f0, wd = RANGES[r]
             per = 512 // wd
-            o = work.tile([128, per, wd], F32, name="o", tag="o", bufs=6)
+            o = work.tile([128, per, wd], F32, name="o", tag="o", bufs=5)
             take(eng, o[:].rearrange("p a f -> p (a f)"), banks["o", f0, k][:])
             nc.sync.dma_start(
                 out=out.rearrange("(k a p) f -> k p a f", a=per, p=128)[k, :, :, f0 : f0 + wd],
                 in_=o[:],
             )
 
-        lay_y(0, 0, "V")
+        prep_gain()
         turn_x12(0, 0, 0)
-        turn_scale(1)
         take_x12(0, 0, 0, "S")
-        quant_y(0, 0)
         turn_x12(0, 0, 1)
-        take_scale(1, "S")
-        quant_x12(0, 0, 0)
-        turn_scale(0)
         take_x12(0, 0, 1, "S")
-        lay_y(1, 0, "V")
-        mm_p(0, 0, 0, 1)
+        turn_scale(0)
         take_scale(0, "S")
-        mm_p(0, 0, 0, 0)
-        act_p(0, 0, 0, 1)
-        turn_x12(1, 0, 1)
-        quant_x12(0, 0, 1)
-        act_p(0, 0, 0, 0)
-        quant_y(1, 0)
+        turn_scale(1)
+        take_scale(1, "S")
+        lay_y(0, 0, "V")
+        quant_y(0, 0)
+        quant_x12(0, 0, 0)
         turn_x12(1, 0, 0)
-        take_x12(1, 0, 1, "S")
-        mm_p(0, 0, 0, 2)
-        scale_x(0)
         take_x12(1, 0, 0, "S")
-        mm_p(0, 0, 0, 3)
-        act_p(0, 0, 0, 2)
-        quant_x12(1, 0)
-        turn_x12(0, 1, 0)
-        act_p(0, 0, 0, 3)
-        scale_x(1)
-        turn_x12(0, 1, 1)
-        take_x12(0, 1, 0, "S")
-        mm_p(1, 0, 0, 0)
-        take_x12(0, 1, 1, "S")
-        mm_p(1, 0, 0, 1)
+        turn_x12(1, 0, 1)
+        take_x12(1, 0, 1, "S")
+        lay_y(1, 0, "V")
+        quant_y(1, 0)
+        quant_x12(0, 0, 1)
         scale_x(2)
-        turn_x(1)
-        act_p(1, 0, 0, 0)
-        mm_p(1, 0, 0, 2)
-        act_p(1, 0, 0, 1)
-        quant_x12(0, 1)
-        turn_x12(1, 1, 1)
-        take_x(1, "S")
-        mul_q(0, 0, 0)
+        turn_x12(0, 1, 0)
+        take_x12(0, 1, 0, "S")
+        turn_x12(0, 1, 1)
+        take_x12(0, 1, 1, "S")
         turn_x12(1, 1, 0)
-        act_p(1, 0, 0, 2)
-        take_x12(1, 1, 1, "V")
-        mm_p(1, 0, 0, 3)
         take_x12(1, 1, 0, "S")
-        mul_q(0, 0, 1)
+        quant_x12(1, 0)
+        scale_x(0)
+        scale_x(3)
+        mm_p(0, 0, 0, 0)
+        mm_p(1, 0, 0, 0)
+        scale_x(1)
+        mm_p(0, 0, 0, 1)
+        mm_p(1, 0, 0, 1)
+        act_p(0, 0, 0, 0)
+        act_p(1, 0, 0, 0)
+        quant_x12(0, 1)
+        mm_p(0, 0, 0, 2)
+        mm_p(1, 0, 0, 2)
+        act_p(0, 0, 0, 1)
+        act_p(1, 0, 0, 1)
+        mul_q(0, 0, 0)
+        turn_x12(1, 1, 1)
+        take_x12(1, 1, 1, "S")
         turn_x(0)
+        take_x(0, "S")
+        mm_p(0, 0, 0, 3)
+        mm_p(1, 0, 0, 3)
+        act_p(0, 0, 0, 2)
+        act_p(1, 0, 0, 2)
+        mul_q(0, 0, 1)
+        quant_x12(1, 1)
+        scale_x(5)
+        scale_x(7)
+        mm_p(0, 1, 0, 0)
+        mm_p(1, 1, 0, 0)
+        act_p(0, 0, 0, 3)
         act_p(1, 0, 0, 3)
         mul_q(0, 0, 2)
-        mm_p(0, 1, 0, 0)
-        take_x(0, "S")
-        mm_p(0, 1, 0, 1)
-        quant_x12(1, 1)
-        mm_g(0, 0, 1)
-        act_p(0, 1, 0, 0)
-        mul_q(0, 0, 3)
-        mm_g(0, 0, 2)
-        mm_p(1, 1, 0, 1)
-        act_p(0, 1, 0, 1)
-        scale_x(3)
-        mm_p(1, 1, 0, 0)
-        mm_g(0, 0, 0)
-        act_p(1, 1, 0, 1)
-        turn_x(2)
-        act_p(1, 1, 0, 0)
-        add_w(0, 0, 1)
-        turn_x(3)
-        take_x(2, "S")
-        add_w(0, 0, 0)
-        mm_g(0, 0, 3)
-        lay_y(1, 1, "S")
-        mm_p(0, 1, 0, 2)
-        mul_q(1, 0, 1)
-        mm_p(1, 1, 0, 2)
-        mm_p(1, 1, 0, 3)
-        add_w(0, 0, 3)
-        mm_p(0, 1, 0, 3)
-        act_p(1, 1, 0, 2)
-        mm_g(1, 0, 0)
-        add_w(0, 0, 2)
-        mm_g(1, 0, 1)
         lay_y(0, 1, "S")
-        mm_g(1, 1, 1)
-        quant_y(1, 1)
-        mm_g(0, 1, 1)
-        quant_w(0, 0)
-        act_p(0, 1, 0, 2)
-        scale_x(4)
-        act_p(1, 1, 0, 3)
-        mm_p(1, 0, 1, 0)
-        quant_y(0, 1)
-        take_x(3, "S")
-        mm_p(1, 0, 1, 1)
-        mul_q(1, 0, 2)
-        act_p(0, 1, 0, 3)
-        turn_x(4)
-        quant_x(0, 0)
-        act_p(1, 0, 1, 1)
-        mm_p(0, 0, 1, 0)
-        quant_x(0, 1)
-        take_x(4, "S")
-        mm_p(0, 1, 1, 0)
-        scale_x(6)
-        act_p(0, 0, 1, 0)
-        mm_g(1, 0, 3)
-        act_p(0, 1, 1, 0)
-        mm_p(1, 1, 1, 0)
-        mul_q(1, 0, 0)
-        act_p(1, 0, 1, 0)
-        turn_x(6)
-        scale_x(7)
-        act_p(1, 1, 1, 0)
-        mm_p(0, 0, 1, 1)
-        take_x(6, "S")
-        mm_g(0, 1, 0)
-        mul_q(0, 1, 0)
+        mm_p(0, 1, 0, 1)
+        mm_p(1, 1, 0, 1)
+        act_p(0, 1, 0, 0)
+        act_p(1, 1, 0, 0)
+        mul_q(0, 0, 3)
+        lay_y(1, 1, "V")
         lay_y(1, 2, "S")
-        turn_x(7)
-        scale_x(5)
-        take_x(7, "S")
-        mul_q(1, 0, 3)
-        lay_y(0, 2, "S")
-        turn_x(5)
+        scale_x(6)
+        mm_g(0, 0, 0)
+        mm_p(0, 1, 0, 2)
+        mm_p(1, 1, 0, 2)
+        act_p(0, 1, 0, 1)
+        act_p(1, 1, 0, 1)
+        mul_q(1, 0, 0)
+        add_w(0, 0, 0)
+        quant_y(0, 1)
+        quant_y(1, 1)
         quant_y(1, 2)
-        add_w(1, 0, 1)
-        add_w(1, 0, 3)
-        mm_p(1, 1, 1, 1)
-        take_x(5, "S")
-        quant_y(0, 2)
-        act_p(0, 0, 1, 1)
-        mm_p(1, 0, 2, 0)
-        add_w(1, 0, 0)
-        mm_p(0, 1, 1, 1)
-        act_p(1, 1, 1, 1)
-        mm_p(0, 0, 2, 1)
-        mul_q(0, 1, 1)
-        mm_g(1, 1, 0)
-        act_p(0, 1, 1, 1)
+        mm_g(0, 0, 2)
+        mm_p(0, 1, 0, 3)
+        mm_p(1, 1, 0, 3)
+        act_p(0, 1, 0, 2)
+        act_p(1, 1, 0, 2)
+        mul_q(1, 0, 1)
+        add_w(0, 0, 2)
+        scale_x(4)
+        turn_x(2)
+        take_x(2, "S")
+        mm_g(0, 0, 1)
+        mm_p(0, 0, 1, 0)
+        mm_p(1, 0, 1, 0)
+        act_p(0, 1, 0, 3)
+        act_p(1, 1, 0, 3)
+        mul_q(1, 0, 2)
+        add_w(0, 0, 1)
+        lay_y(0, 2, "S")
+        turn_x(3)
+        take_x(3, "S")
+        mm_g(0, 0, 3)
+        mm_g(1, 0, 0)
         mm_g(1, 0, 2)
-        quant_x(1, 1)
-        act_p(0, 0, 2, 1)
-        mm_p(1, 0, 2, 1)
+        mm_p(0, 0, 1, 1)
+        mm_p(1, 0, 1, 1)
+        act_p(0, 0, 1, 0)
+        act_p(1, 0, 1, 0)
+        mul_q(1, 0, 3)
+        add_w(0, 0, 3)
+        add_w(1, 0, 0)
         add_w(1, 0, 2)
-        act_p(1, 0, 2, 0)
-        mm_p(1, 1, 2, 0)
-        add_w(0, 1, 0)
-        act_p(1, 0, 2, 1)
-        mm_p(0, 1, 2, 0)
-        mm_g(1, 2, 0)
-        act_p(0, 1, 2, 0)
-        quant_w(1, 0)
+        quant_y(0, 2)
+        mm_g(1, 0, 1)
+        mm_p(0, 1, 1, 0)
+        mm_p(1, 1, 1, 0)
+        act_p(0, 0, 1, 1)
+        act_p(1, 0, 1, 1)
+        mul_q(0, 1, 0)
+        add_w(1, 0, 1)
+        turn_x(1)
+        take_x(1, "S")
+        turn_x(7)
+        take_x(7, "S")
+        mm_g(1, 0, 3)
+        mm_p(0, 1, 1, 1)
+        mm_p(1, 1, 1, 1)
+        act_p(0, 1, 1, 0)
+        act_p(1, 1, 1, 0)
+        mul_q(0, 1, 1)
+        add_w(1, 0, 3)
+        quant_w(0, 0)
+        turn_x(4)
+        take_x(4, "S")
+        turn_x(5)
+        take_x(5, "S")
+        quant_x(0)
         mm_p(0, 0, 2, 0)
-        mm_g(0, 2, 0)
-        act_p(1, 1, 2, 0)
-        quant_x(1, 0)
-        mm_out(0, 0)
-        act_p(0, 0, 2, 0)
-        add_w(0, 1, 1)
-        mm_out(0, 1)
-        take_out(0, 0, "S")
+        mm_p(1, 0, 2, 0)
+        act_p(0, 1, 1, 1)
+        act_p(1, 1, 1, 1)
         mul_q(1, 1, 0)
-        mm_out(0, 4)
-        take_out(0, 1, "S")
-        quant_w(0, 1)
-        mm_out(0, 2)
-        take_out(0, 4, "S")
+        quant_w(1, 0)
+        mm_g(0, 1, 1)
+        mm_g(1, 1, 0)
+        mm_g(1, 1, 1)
+        mm_p(0, 1, 2, 0)
+        mm_p(1, 1, 2, 0)
+        act_p(0, 0, 2, 0)
+        act_p(1, 0, 2, 0)
         mul_q(1, 1, 1)
-        mm_out(0, 3)
-        take_out(0, 2, "S")
-        mul_q(0, 2, 0)
-        mm_out(0, 5)
-        take_out(0, 3, "S")
+        add_w(0, 1, 1)
         add_w(1, 1, 0)
-        mm_out(0, 7)
-        take_out(0, 5, "S")
         add_w(1, 1, 1)
-        mm_p(0, 1, 2, 1)
-        take_out(0, 7, "S")
-        mm_g(1, 2, 1)
-        mm_g(0, 2, 1)
-        mul_q(0, 2, 1)
-        act_p(0, 1, 2, 1)
-        mm_p(1, 1, 2, 1)
+        turn_x(6)
+        take_x(6, "S")
+        quant_x(1)
+        mm_g(0, 1, 0)
+        mm_out(0, 0)
+        take_out(0, 0, "S")
+        mm_out(0, 2)
+        take_out(0, 2, "S")
+        mm_p(0, 0, 3, 0)
+        mm_p(1, 0, 3, 0)
+        act_p(0, 1, 2, 0)
+        act_p(1, 1, 2, 0)
+        mul_q(0, 2, 0)
+        add_w(0, 1, 0)
         quant_w(1, 1)
-        mm_out(0, 6)
-        act_p(1, 1, 2, 1)
-        add_w(0, 2, 1)
-        mm_out(1, 1)
-        take_out(0, 6, "S")
+        mm_g(0, 2, 0)
+        mm_g(1, 2, 0)
+        mm_p(0, 1, 3, 0)
+        mm_p(1, 1, 3, 0)
+        act_p(0, 0, 3, 0)
+        act_p(1, 0, 3, 0)
         mul_q(1, 2, 0)
-        mm_out(1, 0)
-        take_out(1, 1, "S")
         add_w(0, 2, 0)
-        mm_out(1, 2)
-        take_out(1, 0, "S")
-        mul_q(1, 2, 1)
-        mm_out(1, 3)
-        take_out(1, 2, "S")
-        quant_w(0, 2)
-        take_out(1, 3, "S")
         add_w(1, 2, 0)
-        add_w(1, 2, 1)
+        quant_w(0, 1)
+        mm_out(0, 1)
+        take_out(0, 1, "S")
+        mm_out(0, 5)
+        take_out(0, 5, "S")
+        mm_out(0, 7)
+        take_out(0, 7, "S")
+        act_p(0, 1, 3, 0)
+        act_p(1, 1, 3, 0)
+        mul_q(0, 3, 0)
+        quant_w(0, 2)
         quant_w(1, 2)
+        mul_q(1, 3, 0)
+        mm_g(0, 3, 0)
+        mm_g(1, 3, 0)
+        mm_out(0, 3)
+        take_out(0, 3, "S")
+        mm_out(0, 4)
+        take_out(0, 4, "S")
+        mm_out(0, 6)
+        take_out(0, 6, "S")
+        mm_out(1, 0)
+        take_out(1, 0, "S")
+        mm_out(1, 1)
+        take_out(1, 1, "S")
+        add_w(0, 3, 0)
+        add_w(1, 3, 0)
+        quant_w(0, 3)
+        quant_w(1, 3)
         mm_out(2, 0)
-        mm_out(2, 1)
         take_out(2, 0, "S")
-        mm_out(2, 2)
-        take_out(2, 1, "S")
-        mm_out(2, 3)
-        take_out(2, 2, "S")
-        take_out(2, 3, "S")
+        mm_out(1, 2)
+        take_out(1, 2, "S")
+        mm_out(1, 3)
+        take_out(1, 3, "V")
+        mm_out(2, 1)
+        take_out(2, 1, "V")
+        mm_out(3, 0)
+        take_out(3, 0, "V")
+        mm_out(3, 1)
+        take_out(3, 1, "S")

@@ -16,7 +16,8 @@ ACT = mybir.ActivationFunctionType
 ALU = mybir.AluOpType
 
 YPARTS = [(0, 512), (512, 256), (768, 256)]
-RANGES = [(0, 512), (512, 256), (768, 128), (896, 128)]
+OPARTS = [(0, 512, 0), (512, 256, 1), (768, 128, 2), (896, 128, 2)]
+RANGES = [(0, 512), (512, 256), (768, 256)]
 
 
 def tile_fedparatanhhadamardlinear_kernel(
@@ -64,11 +65,6 @@ def tile_fedparatanhhadamardlinear_kernel(
         identb = keep.tile([128, 128], BF16, name="identb")
         make_identity(nc, identb[:])
 
-        zeros = keep.tile([128, 512], BF16, name="zeros")
-        nc.vector.memset(zeros[:], 0.0)
-        idle = bank()
-        for n in range(6):
-            nc.tensor.matmul(idle[:], lhsT=zeros[:, 0:128], rhs=zeros[:], start=True, stop=True)
         xs_t = keep.tile([128, 1024], F32, name="xs_t")
         y_raw = {}
         xr = {}
@@ -369,16 +365,17 @@ def tile_fedparatanhhadamardlinear_kernel(
                 op=ALU.add,
             )
 
-        def quant_w(g, r):
-            f0, wd = RANGES[r]
+        def quant_w(g, p):
+            f0, wd, r = OPARTS[p]
+            o = 4 * (f0 - RANGES[r][0])
             nc.vector.quantize_mx(
                 out=wc[:, g, f0 : f0 + wd].bitcast(FP8X4),
                 scales=ws[:, g, f0 : f0 + wd],
-                in_=wb[g, f0][:],
+                in_=wb[g, RANGES[r][0]][:, o : o + 4 * wd],
             )
 
         def mm_out(r, k):
-            f0, wd = RANGES[r]
+            f0, wd = OPARTS[r][:2]
             per = 512 // wd
             pb = bank()
             for a in range(per):
@@ -396,7 +393,7 @@ def tile_fedparatanhhadamardlinear_kernel(
             banks["o", f0, k] = pb
 
         def take_out(r, k, eng):
-            f0, wd = RANGES[r]
+            f0, wd = OPARTS[r][:2]
             per = 512 // wd
             o = work.tile([128, per, wd], F32, name="o", tag="o", bufs=5)
             take(eng, o[:].rearrange("p a f -> p (a f)"), banks["o", f0, k][:])
@@ -408,8 +405,6 @@ def tile_fedparatanhhadamardlinear_kernel(
         prep_gain()
         turn_x12(0, 0, 0)
         take_x12(0, 0, 0, "S")
-        turn_x12(0, 0, 1)
-        take_x12(0, 0, 1, "S")
         turn_scale(0)
         take_scale(0, "S")
         turn_scale(1)
@@ -417,6 +412,8 @@ def tile_fedparatanhhadamardlinear_kernel(
         lay_y(0, 0, "V")
         quant_y(0, 0)
         quant_x12(0, 0, 0)
+        turn_x12(0, 0, 1)
+        take_x12(0, 0, 1, "S")
         turn_x12(1, 0, 0)
         take_x12(1, 0, 0, "S")
         turn_x12(1, 0, 1)
@@ -424,7 +421,8 @@ def tile_fedparatanhhadamardlinear_kernel(
         lay_y(1, 0, "V")
         quant_y(1, 0)
         quant_x12(0, 0, 1)
-        scale_x(2)
+        scale_x(1)
+        scale_x(3)
         turn_x12(0, 1, 0)
         take_x12(0, 1, 0, "S")
         turn_x12(0, 1, 1)
@@ -433,46 +431,43 @@ def tile_fedparatanhhadamardlinear_kernel(
         take_x12(1, 1, 0, "S")
         quant_x12(1, 0)
         scale_x(0)
-        scale_x(3)
+        scale_x(2)
         mm_p(0, 0, 0, 0)
         mm_p(1, 0, 0, 0)
-        scale_x(1)
         mm_p(0, 0, 0, 1)
         mm_p(1, 0, 0, 1)
         act_p(0, 0, 0, 0)
         act_p(1, 0, 0, 0)
+        turn_x12(1, 1, 1)
+        take_x12(1, 1, 1, "S")
         quant_x12(0, 1)
         mm_p(0, 0, 0, 2)
         mm_p(1, 0, 0, 2)
         act_p(0, 0, 0, 1)
         act_p(1, 0, 0, 1)
         mul_q(0, 0, 0)
-        turn_x12(1, 1, 1)
-        take_x12(1, 1, 1, "S")
-        turn_x(0)
-        take_x(0, "S")
+        quant_x12(1, 1)
+        scale_x(5)
         mm_p(0, 0, 0, 3)
         mm_p(1, 0, 0, 3)
         act_p(0, 0, 0, 2)
         act_p(1, 0, 0, 2)
         mul_q(0, 0, 1)
-        quant_x12(1, 1)
-        scale_x(5)
-        scale_x(7)
         mm_p(0, 1, 0, 0)
         mm_p(1, 1, 0, 0)
         act_p(0, 0, 0, 3)
         act_p(1, 0, 0, 3)
         mul_q(0, 0, 2)
-        lay_y(0, 1, "S")
+        scale_x(4)
         mm_p(0, 1, 0, 1)
         mm_p(1, 1, 0, 1)
         act_p(0, 1, 0, 0)
         act_p(1, 1, 0, 0)
         mul_q(0, 0, 3)
-        lay_y(1, 1, "V")
-        lay_y(1, 2, "S")
+        turn_y(1, 1, 0)
+        take_y(1, 1, 0, "S")
         scale_x(6)
+        scale_x(7)
         mm_g(0, 0, 0)
         mm_p(0, 1, 0, 2)
         mm_p(1, 1, 0, 2)
@@ -480,9 +475,10 @@ def tile_fedparatanhhadamardlinear_kernel(
         act_p(1, 1, 0, 1)
         mul_q(1, 0, 0)
         add_w(0, 0, 0)
+        turn_y(0, 1, 0)
+        take_y(0, 1, 0, "S")
         quant_y(0, 1)
         quant_y(1, 1)
-        quant_y(1, 2)
         mm_g(0, 0, 2)
         mm_p(0, 1, 0, 3)
         mm_p(1, 1, 0, 3)
@@ -490,134 +486,139 @@ def tile_fedparatanhhadamardlinear_kernel(
         act_p(1, 1, 0, 2)
         mul_q(1, 0, 1)
         add_w(0, 0, 2)
-        scale_x(4)
+        turn_y(0, 2, 0)
+        take_y(0, 2, 0, "S")
+        turn_y(1, 2, 0)
+        take_y(1, 2, 0, "S")
+        quant_y(0, 2)
         turn_x(2)
         take_x(2, "S")
-        mm_g(0, 0, 1)
         mm_p(0, 0, 1, 0)
         mm_p(1, 0, 1, 0)
         act_p(0, 1, 0, 3)
         act_p(1, 1, 0, 3)
         mul_q(1, 0, 2)
-        add_w(0, 0, 1)
-        lay_y(0, 2, "S")
-        turn_x(3)
-        take_x(3, "S")
-        mm_g(0, 0, 3)
-        mm_g(1, 0, 0)
-        mm_g(1, 0, 2)
+        quant_y(1, 2)
+        turn_x(1)
+        take_x(1, "S")
+        mm_g(0, 0, 1)
         mm_p(0, 0, 1, 1)
         mm_p(1, 0, 1, 1)
         act_p(0, 0, 1, 0)
         act_p(1, 0, 1, 0)
         mul_q(1, 0, 3)
-        add_w(0, 0, 3)
-        add_w(1, 0, 0)
-        add_w(1, 0, 2)
-        quant_y(0, 2)
+        add_w(0, 0, 1)
+        turn_x(6)
+        take_x(6, "S")
         mm_g(1, 0, 1)
+        mm_g(1, 0, 2)
         mm_p(0, 1, 1, 0)
         mm_p(1, 1, 1, 0)
         act_p(0, 0, 1, 1)
         act_p(1, 0, 1, 1)
         mul_q(0, 1, 0)
         add_w(1, 0, 1)
-        turn_x(1)
-        take_x(1, "S")
-        turn_x(7)
-        take_x(7, "S")
-        mm_g(1, 0, 3)
+        add_w(1, 0, 2)
+        turn_x(4)
+        take_x(4, "S")
+        turn_x(5)
+        take_x(5, "S")
+        mm_g(0, 0, 3)
+        mm_g(1, 0, 0)
         mm_p(0, 1, 1, 1)
         mm_p(1, 1, 1, 1)
         act_p(0, 1, 1, 0)
         act_p(1, 1, 1, 0)
         mul_q(0, 1, 1)
-        add_w(1, 0, 3)
-        quant_w(0, 0)
-        turn_x(4)
-        take_x(4, "S")
-        turn_x(5)
-        take_x(5, "S")
-        quant_x(0)
+        add_w(0, 0, 3)
+        add_w(1, 0, 0)
+        mm_g(1, 0, 3)
         mm_p(0, 0, 2, 0)
         mm_p(1, 0, 2, 0)
         act_p(0, 1, 1, 1)
         act_p(1, 1, 1, 1)
         mul_q(1, 1, 0)
-        quant_w(1, 0)
+        add_w(1, 0, 3)
+        quant_w(0, 0)
         mm_g(0, 1, 1)
-        mm_g(1, 1, 0)
-        mm_g(1, 1, 1)
-        mm_p(0, 1, 2, 0)
-        mm_p(1, 1, 2, 0)
+        mm_p(0, 0, 2, 1)
+        mm_p(1, 0, 2, 1)
         act_p(0, 0, 2, 0)
         act_p(1, 0, 2, 0)
         mul_q(1, 1, 1)
         add_w(0, 1, 1)
-        add_w(1, 1, 0)
-        add_w(1, 1, 1)
-        turn_x(6)
-        take_x(6, "S")
+        quant_w(1, 0)
+        turn_x(0)
+        take_x(0, "S")
+        turn_x(3)
+        take_x(3, "S")
+        turn_x(7)
+        take_x(7, "S")
+        quant_x(0)
         quant_x(1)
+        mm_g(1, 1, 1)
+        mm_p(0, 1, 2, 0)
+        mm_p(1, 1, 2, 0)
+        act_p(0, 0, 2, 1)
+        act_p(1, 0, 2, 1)
+        mul_q(0, 2, 0)
+        add_w(1, 1, 1)
         mm_g(0, 1, 0)
-        mm_out(0, 0)
-        take_out(0, 0, "S")
-        mm_out(0, 2)
-        take_out(0, 2, "S")
-        mm_p(0, 0, 3, 0)
-        mm_p(1, 0, 3, 0)
+        mm_p(0, 1, 2, 1)
+        mm_p(1, 1, 2, 1)
         act_p(0, 1, 2, 0)
         act_p(1, 1, 2, 0)
-        mul_q(0, 2, 0)
+        mul_q(0, 2, 1)
         add_w(0, 1, 0)
+        mm_g(1, 1, 0)
+        mm_out(0, 0)
+        take_out(0, 0, "S")
+        mm_out(0, 1)
+        take_out(0, 1, "S")
+        mm_out(0, 3)
+        take_out(0, 3, "S")
+        mm_out(0, 7)
+        take_out(0, 7, "S")
+        act_p(0, 1, 2, 1)
+        act_p(1, 1, 2, 1)
+        mul_q(1, 2, 0)
+        add_w(1, 1, 0)
+        quant_w(0, 1)
         quant_w(1, 1)
         mm_g(0, 2, 0)
         mm_g(1, 2, 0)
-        mm_p(0, 1, 3, 0)
-        mm_p(1, 1, 3, 0)
-        act_p(0, 0, 3, 0)
-        act_p(1, 0, 3, 0)
-        mul_q(1, 2, 0)
+        mul_q(1, 2, 1)
         add_w(0, 2, 0)
         add_w(1, 2, 0)
-        quant_w(0, 1)
-        mm_out(0, 1)
-        take_out(0, 1, "S")
-        mm_out(0, 5)
-        take_out(0, 5, "S")
-        mm_out(0, 7)
-        take_out(0, 7, "S")
-        act_p(0, 1, 3, 0)
-        act_p(1, 1, 3, 0)
-        mul_q(0, 3, 0)
         quant_w(0, 2)
+        mm_out(0, 2)
+        take_out(0, 2, "S")
         quant_w(1, 2)
-        mul_q(1, 3, 0)
-        mm_g(0, 3, 0)
-        mm_g(1, 3, 0)
-        mm_out(0, 3)
-        take_out(0, 3, "S")
+        mm_g(0, 2, 1)
         mm_out(0, 4)
         take_out(0, 4, "S")
+        mm_out(0, 5)
+        take_out(0, 5, "S")
+        add_w(0, 2, 1)
+        mm_g(1, 2, 1)
         mm_out(0, 6)
         take_out(0, 6, "S")
-        mm_out(1, 0)
-        take_out(1, 0, "S")
         mm_out(1, 1)
         take_out(1, 1, "S")
-        add_w(0, 3, 0)
-        add_w(1, 3, 0)
-        quant_w(0, 3)
-        quant_w(1, 3)
-        mm_out(2, 0)
-        take_out(2, 0, "S")
         mm_out(1, 2)
         take_out(1, 2, "S")
+        add_w(1, 2, 1)
+        quant_w(0, 3)
+        quant_w(1, 3)
+        mm_out(1, 0)
+        take_out(1, 0, "S")
         mm_out(1, 3)
-        take_out(1, 3, "V")
+        take_out(1, 3, "S")
+        mm_out(2, 0)
+        take_out(2, 0, "V")
         mm_out(2, 1)
         take_out(2, 1, "V")
         mm_out(3, 0)
-        take_out(3, 0, "V")
+        take_out(3, 0, "S")
         mm_out(3, 1)
         take_out(3, 1, "S")

@@ -315,7 +315,7 @@ def tile_fedparatanhhadamardlinear_kernel(
                 a = work.tile([128, 512], F32, name="t1", tag="t1", bufs=6)
                 nc.scalar.activation(a[:], pb[:], ACT.Tanh)
             else:
-                a = work.tile([128, 512], F32, name="s2", tag="s2", bufs=6)
+                a = work.tile([128, 512], F32, name="s2", tag="s2", bufs=5)
                 nc.scalar.activation(a[:], pb[:], ACT.Sigmoid, scale=2.0)
             pt[w, g, f0, j] = a
 
@@ -326,7 +326,9 @@ def tile_fedparatanhhadamardlinear_kernel(
             f0, wd = RANGES[r]
             per = 512 // wd
             if (g, f0) not in qt:
-                q = work.tile([128, 4, wd], F32, name="qt", tag="qt", bufs=3)
+                q = work.tile(
+                    [128, 4, wd], F32, name="qt", tag="qt%d" % wd, bufs=2 if wd == 512 else 4
+                )
                 qt[g, f0] = q
             for a in range(per):
                 t = j * per + a
@@ -356,7 +358,7 @@ def tile_fedparatanhhadamardlinear_kernel(
         def add_w(g, r, n):
             f0, wd = RANGES[r]
             if (g, f0) not in wb:
-                t = work.tile([128, 4 * wd], BF16, name="wb", tag="wb", bufs=3, align_bytes=256)
+                t = work.tile([128, 4 * wd], BF16, name="wb", tag="wb%d" % wd, bufs=2, align_bytes=256)
                 wb[g, f0] = t
             nc.vector.tensor_tensor(
                 out=wb[g, f0][:, 512 * n : 512 * n + 512].rearrange("p (n t) -> p n t", t=4),
@@ -395,16 +397,17 @@ def tile_fedparatanhhadamardlinear_kernel(
         def take_out(r, k, eng):
             f0, wd = OPARTS[r][:2]
             per = 512 // wd
-            o = work.tile([128, per, wd], F32, name="o", tag="o", bufs=5)
+            o = work.tile([128, per, wd], F32, name="o", tag="o", bufs=4)
             take(eng, o[:].rearrange("p a f -> p (a f)"), banks["o", f0, k][:])
             nc.sync.dma_start(
                 out=out.rearrange("(k a p) f -> k p a f", a=per, p=128)[k, :, :, f0 : f0 + wd],
                 in_=o[:],
             )
 
-        prep_gain()
         turn_x12(0, 0, 0)
         take_x12(0, 0, 0, "S")
+        turn_x12(0, 0, 1)
+        take_x12(0, 0, 1, "S")
         turn_scale(0)
         take_scale(0, "S")
         turn_scale(1)
@@ -412,15 +415,15 @@ def tile_fedparatanhhadamardlinear_kernel(
         lay_y(0, 0, "V")
         quant_y(0, 0)
         quant_x12(0, 0, 0)
-        turn_x12(0, 0, 1)
-        take_x12(0, 0, 1, "S")
+        prep_gain()
+        lay_y(1, 0, "V")
+        quant_y(1, 0)
+        quant_x12(0, 0, 1)
+        scale_x(2)
         turn_x12(1, 0, 0)
         take_x12(1, 0, 0, "S")
         turn_x12(1, 0, 1)
         take_x12(1, 0, 1, "S")
-        lay_y(1, 0, "V")
-        quant_y(1, 0)
-        quant_x12(0, 0, 1)
         scale_x(1)
         scale_x(3)
         turn_x12(0, 1, 0)
@@ -429,177 +432,175 @@ def tile_fedparatanhhadamardlinear_kernel(
         take_x12(0, 1, 1, "S")
         turn_x12(1, 1, 0)
         take_x12(1, 1, 0, "S")
-        quant_x12(1, 0)
-        scale_x(0)
-        scale_x(2)
-        mm_p(0, 0, 0, 0)
-        mm_p(1, 0, 0, 0)
-        mm_p(0, 0, 0, 1)
-        mm_p(1, 0, 0, 1)
-        act_p(0, 0, 0, 0)
-        act_p(1, 0, 0, 0)
         turn_x12(1, 1, 1)
         take_x12(1, 1, 1, "S")
-        quant_x12(0, 1)
+        quant_x12(1, 0)
+        scale_x(0)
         mm_p(0, 0, 0, 2)
-        mm_p(1, 0, 0, 2)
-        act_p(0, 0, 0, 1)
-        act_p(1, 0, 0, 1)
-        mul_q(0, 0, 0)
-        quant_x12(1, 1)
-        scale_x(5)
         mm_p(0, 0, 0, 3)
         mm_p(1, 0, 0, 3)
         act_p(0, 0, 0, 2)
-        act_p(1, 0, 0, 2)
-        mul_q(0, 0, 1)
-        mm_p(0, 1, 0, 0)
-        mm_p(1, 1, 0, 0)
         act_p(0, 0, 0, 3)
         act_p(1, 0, 0, 3)
-        mul_q(0, 0, 2)
-        scale_x(4)
+        quant_x12(0, 1)
+        quant_x12(1, 1)
+        scale_x(5)
         mm_p(0, 1, 0, 1)
-        mm_p(1, 1, 0, 1)
-        act_p(0, 1, 0, 0)
-        act_p(1, 1, 0, 0)
-        mul_q(0, 0, 3)
-        turn_y(1, 1, 0)
-        take_y(1, 1, 0, "S")
-        scale_x(6)
-        scale_x(7)
-        mm_g(0, 0, 0)
         mm_p(0, 1, 0, 2)
+        mm_p(0, 1, 0, 3)
+        mm_p(1, 0, 0, 0)
+        mm_p(1, 0, 0, 2)
         mm_p(1, 1, 0, 2)
+        mul_q(0, 0, 3)
+        scale_x(4)
+        scale_x(6)
+        mm_p(0, 0, 0, 0)
         act_p(0, 1, 0, 1)
-        act_p(1, 1, 0, 1)
-        mul_q(1, 0, 0)
-        add_w(0, 0, 0)
+        act_p(0, 1, 0, 2)
+        act_p(0, 1, 0, 3)
+        act_p(1, 0, 0, 0)
+        act_p(1, 1, 0, 2)
         turn_y(0, 1, 0)
         take_y(0, 1, 0, "S")
+        turn_y(1, 1, 0)
+        take_y(1, 1, 0, "S")
+        scale_x(7)
+        mm_p(0, 0, 0, 1)
+        mm_p(1, 1, 0, 0)
+        act_p(1, 0, 0, 2)
         quant_y(0, 1)
-        quant_y(1, 1)
-        mm_g(0, 0, 2)
-        mm_p(0, 1, 0, 3)
+        turn_x(6)
+        take_x(6, "V")
+        mm_p(1, 0, 0, 1)
+        act_p(0, 0, 0, 0)
+        act_p(1, 1, 0, 0)
+        mm_p(0, 1, 0, 0)
         mm_p(1, 1, 0, 3)
-        act_p(0, 1, 0, 2)
-        act_p(1, 1, 0, 2)
-        mul_q(1, 0, 1)
-        add_w(0, 0, 2)
-        turn_y(0, 2, 0)
-        take_y(0, 2, 0, "S")
+        mul_q(0, 0, 2)
+        mul_q(1, 0, 2)
+        act_p(0, 0, 0, 1)
+        act_p(1, 0, 0, 1)
+        mul_q(0, 0, 0)
+        quant_y(1, 1)
+        mm_g(0, 0, 0)
+        mm_p(0, 1, 1, 0)
+        mm_p(0, 1, 1, 1)
+        mm_p(1, 1, 0, 1)
+        act_p(0, 1, 0, 0)
+        act_p(1, 1, 0, 3)
+        mul_q(0, 0, 1)
+        mul_q(1, 0, 0)
+        add_w(0, 0, 0)
         turn_y(1, 2, 0)
         take_y(1, 2, 0, "S")
-        quant_y(0, 2)
-        turn_x(2)
-        take_x(2, "S")
-        mm_p(0, 0, 1, 0)
-        mm_p(1, 0, 1, 0)
-        act_p(0, 1, 0, 3)
-        act_p(1, 1, 0, 3)
-        mul_q(1, 0, 2)
-        quant_y(1, 2)
-        turn_x(1)
-        take_x(1, "S")
-        mm_g(0, 0, 1)
-        mm_p(0, 0, 1, 1)
-        mm_p(1, 0, 1, 1)
-        act_p(0, 0, 1, 0)
-        act_p(1, 0, 1, 0)
-        mul_q(1, 0, 3)
-        add_w(0, 0, 1)
-        turn_x(6)
-        take_x(6, "S")
-        mm_g(1, 0, 1)
-        mm_g(1, 0, 2)
-        mm_p(0, 1, 1, 0)
         mm_p(1, 1, 1, 0)
-        act_p(0, 0, 1, 1)
-        act_p(1, 0, 1, 1)
-        mul_q(0, 1, 0)
-        add_w(1, 0, 1)
-        add_w(1, 0, 2)
-        turn_x(4)
-        take_x(4, "S")
-        turn_x(5)
-        take_x(5, "S")
-        mm_g(0, 0, 3)
-        mm_g(1, 0, 0)
-        mm_p(0, 1, 1, 1)
         mm_p(1, 1, 1, 1)
-        act_p(0, 1, 1, 0)
+        act_p(1, 1, 0, 1)
+        quant_y(1, 2)
+        mm_p(0, 0, 1, 0)
         act_p(1, 1, 1, 0)
-        mul_q(0, 1, 1)
-        add_w(0, 0, 3)
-        add_w(1, 0, 0)
-        mm_g(1, 0, 3)
-        mm_p(0, 0, 2, 0)
-        mm_p(1, 0, 2, 0)
-        act_p(0, 1, 1, 1)
         act_p(1, 1, 1, 1)
-        mul_q(1, 1, 0)
-        add_w(1, 0, 3)
-        quant_w(0, 0)
-        mm_g(0, 1, 1)
-        mm_p(0, 0, 2, 1)
-        mm_p(1, 0, 2, 1)
-        act_p(0, 0, 2, 0)
-        act_p(1, 0, 2, 0)
-        mul_q(1, 1, 1)
-        add_w(0, 1, 1)
-        quant_w(1, 0)
-        turn_x(0)
-        take_x(0, "S")
-        turn_x(3)
-        take_x(3, "S")
+        mul_q(1, 0, 3)
         turn_x(7)
         take_x(7, "S")
-        quant_x(0)
-        quant_x(1)
-        mm_g(1, 1, 1)
-        mm_p(0, 1, 2, 0)
-        mm_p(1, 1, 2, 0)
-        act_p(0, 0, 2, 1)
-        act_p(1, 0, 2, 1)
-        mul_q(0, 2, 0)
-        add_w(1, 1, 1)
-        mm_g(0, 1, 0)
+        mm_g(0, 0, 3)
+        mm_g(1, 0, 1)
+        act_p(0, 0, 1, 0)
+        act_p(0, 1, 1, 0)
+        act_p(0, 1, 1, 1)
+        mul_q(1, 0, 1)
+        add_w(0, 0, 3)
+        add_w(1, 0, 1)
+        turn_y(0, 2, 0)
+        take_y(0, 2, 0, "S")
+        mm_g(0, 0, 1)
+        mm_g(1, 0, 2)
+        mm_g(1, 0, 3)
+        mm_p(0, 0, 1, 1)
+        mm_p(1, 0, 1, 1)
+        act_p(1, 0, 1, 1)
+        add_w(0, 0, 1)
+        add_w(1, 0, 2)
+        add_w(1, 0, 3)
+        quant_y(0, 2)
+        mm_g(0, 0, 2)
+        mm_g(1, 0, 0)
+        mm_p(1, 0, 1, 0)
+        act_p(0, 0, 1, 1)
+        act_p(1, 0, 1, 0)
+        mul_q(1, 1, 0)
+        add_w(0, 0, 2)
+        add_w(1, 0, 0)
+        turn_x(0)
+        take_x(0, "S")
+        turn_x(1)
+        take_x(1, "S")
         mm_p(0, 1, 2, 1)
-        mm_p(1, 1, 2, 1)
-        act_p(0, 1, 2, 0)
-        act_p(1, 1, 2, 0)
-        mul_q(0, 2, 1)
-        add_w(0, 1, 0)
-        mm_g(1, 1, 0)
-        mm_out(0, 0)
-        take_out(0, 0, "S")
-        mm_out(0, 1)
-        take_out(0, 1, "S")
-        mm_out(0, 3)
-        take_out(0, 3, "S")
-        mm_out(0, 7)
-        take_out(0, 7, "S")
+        mm_p(1, 1, 2, 0)
         act_p(0, 1, 2, 1)
-        act_p(1, 1, 2, 1)
-        mul_q(1, 2, 0)
+        mul_q(0, 1, 1)
+        mm_p(0, 1, 2, 0)
+        mm_p(1, 0, 2, 0)
+        act_p(0, 1, 2, 0)
+        quant_w(0, 0)
+        turn_x(2)
+        take_x(2, "S")
+        turn_x(3)
+        take_x(3, "S")
+        mm_g(0, 1, 0)
+        mm_p(0, 0, 2, 1)
+        mm_p(1, 0, 2, 1)
+        act_p(1, 0, 2, 0)
+        mul_q(0, 1, 0)
+        mul_q(1, 1, 1)
+        add_w(0, 1, 0)
+        turn_x(5)
+        take_x(5, "S")
+        quant_x(0)
+        mm_g(1, 1, 0)
+        mm_p(0, 0, 2, 0)
+        mm_p(1, 1, 2, 1)
+        act_p(0, 0, 2, 1)
+        act_p(1, 1, 2, 0)
         add_w(1, 1, 0)
+        quant_w(1, 0)
+        turn_x(4)
+        take_x(4, "S")
+        quant_x(1)
+        mm_g(0, 1, 1)
+        mm_g(1, 1, 1)
+        act_p(0, 0, 2, 0)
+        act_p(1, 0, 2, 1)
+        act_p(1, 1, 2, 1)
+        mul_q(0, 2, 0)
+        mul_q(1, 2, 1)
+        add_w(0, 1, 1)
+        add_w(1, 1, 1)
         quant_w(0, 1)
         quant_w(1, 1)
         mm_g(0, 2, 0)
         mm_g(1, 2, 0)
-        mul_q(1, 2, 1)
+        mm_out(0, 1)
+        take_out(0, 1, "S")
+        mm_out(0, 3)
+        take_out(0, 3, "S")
+        mm_out(0, 4)
+        take_out(0, 4, "S")
+        mul_q(0, 2, 1)
+        mul_q(1, 2, 0)
         add_w(0, 2, 0)
         add_w(1, 2, 0)
         quant_w(0, 2)
+        quant_w(1, 2)
+        mm_out(0, 0)
+        take_out(0, 0, "S")
         mm_out(0, 2)
         take_out(0, 2, "S")
-        quant_w(1, 2)
-        mm_g(0, 2, 1)
-        mm_out(0, 4)
-        take_out(0, 4, "S")
         mm_out(0, 5)
         take_out(0, 5, "S")
-        add_w(0, 2, 1)
+        mm_out(0, 7)
+        take_out(0, 7, "S")
+        mm_g(0, 2, 1)
         mm_g(1, 2, 1)
         mm_out(0, 6)
         take_out(0, 6, "S")
@@ -607,6 +608,7 @@ def tile_fedparatanhhadamardlinear_kernel(
         take_out(1, 1, "S")
         mm_out(1, 2)
         take_out(1, 2, "S")
+        add_w(0, 2, 1)
         add_w(1, 2, 1)
         quant_w(0, 3)
         quant_w(1, 3)
@@ -615,7 +617,7 @@ def tile_fedparatanhhadamardlinear_kernel(
         mm_out(1, 3)
         take_out(1, 3, "S")
         mm_out(2, 0)
-        take_out(2, 0, "V")
+        take_out(2, 0, "S")
         mm_out(2, 1)
         take_out(2, 1, "V")
         mm_out(3, 0)

from contextlib import ExitStack

import concourse.mybir as mybir
from concourse.masks import make_identity

T, D, F, R = 1024, 1024, 1024, 512
FLOPS = 2 * 2 * D * R * F + 2 * T * D * F

F32 = mybir.dt.float32
BF16 = mybir.dt.bfloat16
U32 = mybir.dt.uint32
U8 = mybir.dt.uint8
FP8 = mybir.dt.float8_e4m3fn
FP8X4 = mybir.dt.float8_e4m3fn_x4
ACT = mybir.ActivationFunctionType
ALU = mybir.AluOpType

YPARTS = [(0, 512), (512, 256), (768, 256)]
OPARTS = [(0, 512, 0), (512, 256, 1), (768, 128, 2), (896, 128, 2)]
RANGES = [(0, 512), (512, 256), (768, 256)]


def tile_fedparatanhhadamardlinear_kernel(
    tc, x_bytes, x_scale, w0, x1, y1, x2, y2, gain, out
):
    nc = tc.nc
    with ExitStack() as ctx:
        keep = ctx.enter_context(tc.tile_pool(name="keep", bufs=1))
        work = ctx.enter_context(tc.tile_pool(name="work", bufs=2))
        psum = ctx.enter_context(tc.psum_pool(name="psum", bufs=8))
        ctx.enter_context(
            tc.manual_schedule(
                engines={
                    mybir.EngineType.PE,
                    mybir.EngineType.Activation,
                    mybir.EngineType.DVE,
                }
            )
        )

        def bank():
            b = psum.tile([128, 512], F32, name="bank", tag="bank")
            return b

        def take(eng, dst, src):
            if eng == "S":
                nc.scalar.copy(dst, src)
            else:
                nc.vector.tensor_copy(out=dst, in_=src)

        gain_bf = keep.tile([128, 8], BF16, name="gain_bf")
        nc.scalar.dma_start(
            out=gain_bf[:].rearrange("p (g t) -> p g t", g=2),
            in_=gain.rearrange("(g p t) -> p g t", g=2, p=128, t=4),
        )
        scale_kp = keep.tile([128, 8], F32, name="scale_kp")
        nc.scalar.dma_start(
            out=scale_kp[:], in_=x_scale.rearrange("o (m p) -> p (o m)", p=128)
        )
        warm = keep.tile([128, 1], F32, name="warm")
        nc.vector.memset(warm[:], 0.0)
        nc.scalar.activation(warm[:], warm[:], ACT.Sigmoid)
        ident = keep.tile([128, 128], F32, name="ident")
        make_identity(nc, ident[:])
        identb = keep.tile([128, 128], BF16, name="identb")
        make_identity(nc, identb[:])

        xs_t = keep.tile([128, 1024], F32, name="xs_t")
        y_raw = {}
        xr = {}
        w0_raw = {}
        xb = {}

        def load_y(w, r):
            y = y1 if w == 0 else y2
            f0, wd = 512 * r, 512
            t = keep.tile([128, 4, wd], BF16, name="y%d%d" % (w, r))
            nc.sync.dma_start(
                out=t[:], in_=y.rearrange("(p j) f -> p j f", j=4)[:, :, f0 : f0 + wd]
            )
            y_raw[w, r] = t

        def load_x12(w, g, b=None):
            x = x1 if w == 0 else x2
            if (w, g) not in xr:
                t = keep.tile([128, 4, 512], BF16, name="x%d%d" % (w, g))
                xr[w, g] = t
            ts = slice(0, 4) if b is None else slice(2 * b, 2 * b + 2)
            nc.sync.dma_start(
                out=xr[w, g][:, ts, :],
                in_=x.rearrange("(g m t) k -> g m t k", g=2, m=128, t=4)[g][:, ts, :],
            )

        def load_w0(g, r):
            f0, wd = 512 * r, 512
            t = keep.tile([128, 4, wd], BF16, name="w%d%d" % (g, r))
            nc.sync.dma_start(
                out=t[:],
                in_=w0.rearrange("(g m t) f -> g m t f", g=2, m=128, t=4)[
                    g, :, :, f0 : f0 + wd
                ],
            )
            w0_raw[g, r] = t

        def load_x(half):
            t = keep.tile([128, 4, 1024], U8, name="xb%d" % half)
            nc.sync.dma_start(
                out=t[:],
                in_=x_bytes.rearrange("(h i p) d -> h p i d", h=2, i=4, p=128)[half],
            )
            xb[half] = t


        load_y(0, 0)
        load_x12(0, 0, 0)
        load_x12(0, 0, 1)
        load_y(1, 0)
        load_x12(1, 0)
        load_x(0)
        load_x12(0, 1)
        load_x12(1, 1)
        load_w0(0, 0)
        load_w0(1, 0)
        load_x(1)
        load_y(0, 1)
        load_y(1, 1)
        load_w0(0, 1)
        load_w0(1, 1)

        x12c = keep.tile([128, 4, 512], U32, name="x12c", align_bytes=256)
        x12s = keep.tile([128, 4, 512], U8, name="x12s", align_bytes=256)
        yc = keep.tile([128, 2, 1024], U32, name="yc", align_bytes=256)
        ys = keep.tile([128, 2, 1024], U8, name="ys", align_bytes=256)
        xc = keep.tile([128, 2, 2, 512], U32, name="xc", align_bytes=256)
        xsc = keep.tile([128, 2, 2, 512], U8, name="xsc", align_bytes=256)
        wc = keep.tile([128, 2, 1024], U32, name="wc", align_bytes=256)
        ws = keep.tile([128, 2, 1024], U8, name="ws", align_bytes=256)

        banks = {}
        gain_f = keep.tile([128, 8], F32, name="gain_f")
        gain_1 = keep.tile([128, 8], F32, name="gain_1")
        diag = keep.tile([128, 8, 128], BF16, name="diag")

        def prep_gain():
            nc.scalar.copy(gain_f[:], gain_bf[:])
            nc.scalar.activation(gain_1[:], gain_bf[:], ACT.Copy, scale=0.1)
            for j in range(8):
                nc.scalar.activation(
                    diag[:, j, :], identb[:], ACT.Copy, scale=gain_f[:, j : j + 1]
                )

        def turn_scale(b):
            pb = bank()
            for a in range(4):
                m = 4 * b + a
                nc.tensor.transpose(
                    pb[:, 128 * a : 128 * a + 128],
                    scale_kp[:, m : m + 1].to_broadcast([128, 128]),
                    ident[:],
                )
            banks["sc", b] = pb

        def take_scale(b, eng):
            take(eng, xs_t[:, 512 * b : 512 * b + 512], banks["sc", b][:])

        xt12 = {}

        def turn_x12(w, g, b):
            words = xr[w, g][:].rearrange("p t k -> p (t k)").bitcast(F32)
            pb = bank()
            for tt in range(2):
                for u in range(2):
                    o = 256 * (2 * b + tt)
                    nc.tensor.transpose(
                        pb[:, 256 * tt + 128 * u : 256 * tt + 128 * u + 128],
                        words[:, o + u : o + 256 : 2],
                        ident[:],
                    )
            banks["x12", w, g, b] = pb

        def take_x12(w, g, b, eng):
            if (w, g) not in xt12:
                t = work.tile([128, 2048], BF16, name="xt12", tag="xt12", bufs=3, align_bytes=256)
                xt12[w, g] = t
            take(
                eng,
                xt12[w, g][:]
                .bitcast(F32)[:, 512 * b : 512 * b + 512]
                .rearrange("p (t m u) -> p t m u", t=2, m=128),
                banks["x12", w, g, b][:].rearrange("p (t u m) -> p t m u", t=2, u=2),
            )

        def quant_x12(w, g, b=None):
            c = slice(0, 512) if b is None else slice(256 * b, 256 * b + 256)
            i = slice(0, 2048) if b is None else slice(1024 * b, 1024 * b + 1024)
            nc.vector.quantize_mx(
                out=x12c[:, 2 * w + g, c].bitcast(FP8X4),
                scales=x12s[:, 2 * w + g, c],
                in_=xt12[w, g][:, i],
            )

        yg = {}

        def new_yg(w, r):
            if (w, r) not in yg:
                t = work.tile(
                    [128, YPARTS[r][1], 4], BF16, name="yg", tag="yg", bufs=3, align_bytes=256
                )
                yg[w, r] = t
            return yg[w, r]

        def lay_y(w, r, eng):
            take(
                eng,
                new_yg(w, r)[:].rearrange("p (c i) j -> p c j i", i=4),
                y_raw[w, YPARTS[r][0] // 512][
                    :, :, YPARTS[r][0] % 512 : YPARTS[r][0] % 512 + YPARTS[r][1]
                ].rearrange("p j (c i) -> p c j i", i=4),
            )

        def turn_y(w, r, b):
            pb = psum.tile([128, 1024], BF16, name="bank", tag="bank")
            for a in range(2):
                n = YPARTS[r][0] % 512 + 256 * b + 128 * a
                nc.tensor.matmul(
                    pb[:, 512 * a : 512 * a + 512],
                    lhsT=identb[:],
                    rhs=y_raw[w, YPARTS[r][0] // 512][:, :, n : n + 128].rearrange("p j n -> p n j"),
                    start=True,
                    stop=True,
                )
            banks["y", w, r, b] = pb

        def take_y(w, r, b, eng):
            t = new_yg(w, r)
            take(
                eng,
                t[:].rearrange("p f j -> p (f j)").bitcast(F32)[:, 512 * b : 512 * b + 512],
                banks["y", w, r, b][:].bitcast(F32),
            )

        def quant_y(w, r):
            f0, wd = YPARTS[r]
            nc.vector.quantize_mx(
                out=yc[:, w, f0 : f0 + wd].bitcast(FP8X4),
                scales=ys[:, w, f0 : f0 + wd],
                in_=yg[w, r][:].rearrange("p f j -> p (f j)"),
            )

        xw = {}
        xt = {}

        def scale_x(i):
            t = work.tile([128, 1024], BF16, name="xw", tag="xw", bufs=8, align_bytes=256)
            nc.vector.tensor_tensor(
                out=t[:], in0=xb[i // 4][:, i % 4, :].bitcast(FP8), in1=xs_t[:], op=ALU.mult
            )
            xw[i] = t

        def turn_x(i):
            words = xw[i][:].bitcast(F32)
            pb = bank()
            for g in range(2):
                for u in range(2):
                    o = 256 * g + 128 * u
                    nc.tensor.transpose(
                        pb[:, o : o + 128], words[:, 256 * g + u : 256 * g + 256 : 2], ident[:]
                    )
            banks["x", i] = pb

        def take_x(i, eng):
            half = i // 4
            if half not in xt:
                t = work.tile([128, 2, 2048], BF16, name="xt", tag="xt", bufs=2, align_bytes=256)
                xt[half] = t
            r = 256 * (i % 4)
            take(
                eng,
                xt[half][:]
                .bitcast(F32)[:, :, r : r + 256]
                .rearrange("p g (r u) -> p g r u", u=2),
                banks["x", i][:].rearrange("p (g u r) -> p g r u", g=2, u=2),
            )

        def quant_x(half):
            nc.vector.quantize_mx(
                out=xc[:, half, :, :].rearrange("p g r -> p (g r)").bitcast(FP8X4),
                scales=xsc[:, half, :, :].rearrange("p g r -> p (g r)"),
                in_=xt[half][:].rearrange("p g c -> p (g c)"),
            )

        pt = {}

        def mm_p(w, g, r, j):
            f0, wd = RANGES[r]
            per = 512 // wd
            pb = bank()
            for a in range(per):
                t = j * per + a
                nc.tensor.matmul_mx(
                    out=pb[:, a * wd : (a + 1) * wd],
                    lhsT=x12c[:, 2 * w + g, 128 * t : 128 * t + 128].bitcast(FP8X4),
                    lhsT_scale=x12s[:, 2 * w + g, 128 * t : 128 * t + 128],
                    rhs=yc[:, w, f0 : f0 + wd].bitcast(FP8X4),
                    rhs_scale=ys[:, w, f0 : f0 + wd],
                    start=True,
                    stop=True,
                )
            banks["p", w, g, f0, j] = pb

        def act_p(w, g, r, j):
            f0, wd = RANGES[r]
            pb = banks["p", w, g, f0, j]
            if w == 0:
                a = work.tile([128, 512], F32, name="t1", tag="t1", bufs=6)
                nc.scalar.activation(a[:], pb[:], ACT.Tanh)
            else:
                a = work.tile([128, 512], F32, name="s2", tag="s2", bufs=5)
                nc.scalar.activation(a[:], pb[:], ACT.Sigmoid, scale=2.0)
            pt[w, g, f0, j] = a

        qt = {}
        wb = {}

        def mul_q(g, r, j):
            f0, wd = RANGES[r]
            per = 512 // wd
            if (g, f0) not in qt:
                q = work.tile(
                    [128, 4, wd], F32, name="qt", tag="qt%d" % wd, bufs=2 if wd == 512 else 4
                )
                qt[g, f0] = q
            for a in range(per):
                t = j * per + a
                sl = slice(a * wd, (a + 1) * wd)
                nc.vector.scalar_tensor_tensor(
                    out=qt[g, f0][:, t, :],
                    in0=pt[0, g, f0, j][:, sl],
                    scalar=gain_1[:, 4 * g + t : 4 * g + t + 1],
                    in1=pt[1, g, f0, j][:, sl],
                    op0=ALU.mult,
                    op1=ALU.mult,
                )

        def mm_g(g, r, n):
            pb = bank()
            o = RANGES[r][0] % 512 + 128 * n
            for t in range(4):
                nc.tensor.matmul(
                    pb[:, 128 * t : 128 * t + 128],
                    lhsT=diag[:, 4 * g + t, :],
                    rhs=w0_raw[g, RANGES[r][0] // 512][:, t, o : o + 128],
                    start=True,
                    stop=True,
                )
            banks["g", g, r, n] = pb

        def add_w(g, r, n):
            f0, wd = RANGES[r]
            if (g, f0) not in wb:
                t = work.tile([128, 4 * wd], BF16, name="wb", tag="wb%d" % wd, bufs=2, align_bytes=256)
                wb[g, f0] = t
            nc.vector.tensor_tensor(
                out=wb[g, f0][:, 512 * n : 512 * n + 512].rearrange("p (n t) -> p n t", t=4),
                in0=banks["g", g, r, n][:].rearrange("p (t n) -> p n t", t=4),
                in1=qt[g, f0][:, :, 128 * n : 128 * n + 128].rearrange("p t n -> p n t"),
                op=ALU.add,
            )

        def quant_w(g, p):
            f0, wd, r = OPARTS[p]
            o = 4 * (f0 - RANGES[r][0])
            nc.vector.quantize_mx(
                out=wc[:, g, f0 : f0 + wd].bitcast(FP8X4),
                scales=ws[:, g, f0 : f0 + wd],
                in_=wb[g, RANGES[r][0]][:, o : o + 4 * wd],
            )

        def mm_out(r, k):
            f0, wd = OPARTS[r][:2]
            per = 512 // wd
            pb = bank()
            for a in range(per):
                i = k * per + a
                for g in range(2):
                    nc.tensor.matmul_mx(
                        out=pb[:, a * wd : (a + 1) * wd],
                        lhsT=xc[:, i // 4, g, 128 * (i % 4) : 128 * (i % 4) + 128].bitcast(FP8X4),
                        lhsT_scale=xsc[:, i // 4, g, 128 * (i % 4) : 128 * (i % 4) + 128],
                        rhs=wc[:, g, f0 : f0 + wd].bitcast(FP8X4),
                        rhs_scale=ws[:, g, f0 : f0 + wd],
                        start=(g == 0),
                        stop=(g == 1),
                    )
            banks["o", f0, k] = pb

        def take_out(r, k, eng):
            f0, wd = OPARTS[r][:2]
            per = 512 // wd
            o = work.tile([128, per, wd], F32, name="o", tag="o", bufs=4)
            take(eng, o[:].rearrange("p a f -> p (a f)"), banks["o", f0, k][:])
            nc.sync.dma_start(
                out=out.rearrange("(k a p) f -> k p a f", a=per, p=128)[k, :, :, f0 : f0 + wd],
                in_=o[:],
            )

        turn_x12(0, 0, 0)
        take_x12(0, 0, 0, "S")
        turn_x12(0, 0, 1)
        take_x12(0, 0, 1, "S")
        turn_scale(0)
        take_scale(0, "S")
        turn_scale(1)
        take_scale(1, "S")
        lay_y(0, 0, "V")
        quant_y(0, 0)
        quant_x12(0, 0, 0)
        prep_gain()
        lay_y(1, 0, "V")
        quant_y(1, 0)
        quant_x12(0, 0, 1)
        scale_x(2)
        turn_x12(1, 0, 0)
        take_x12(1, 0, 0, "S")
        turn_x12(1, 0, 1)
        take_x12(1, 0, 1, "S")
        scale_x(1)
        scale_x(3)
        turn_x12(0, 1, 0)
        take_x12(0, 1, 0, "S")
        turn_x12(0, 1, 1)
        take_x12(0, 1, 1, "S")
        turn_x12(1, 1, 0)
        take_x12(1, 1, 0, "S")
        turn_x12(1, 1, 1)
        take_x12(1, 1, 1, "S")
        quant_x12(1, 0)
        scale_x(0)
        mm_p(0, 0, 0, 2)
        mm_p(0, 0, 0, 3)
        mm_p(1, 0, 0, 3)
        act_p(0, 0, 0, 2)
        act_p(0, 0, 0, 3)
        act_p(1, 0, 0, 3)
        quant_x12(0, 1)
        quant_x12(1, 1)
        scale_x(5)
        mm_p(0, 1, 0, 1)
        mm_p(0, 1, 0, 2)
        mm_p(0, 1, 0, 3)
        mm_p(1, 0, 0, 0)
        mm_p(1, 0, 0, 2)
        mm_p(1, 1, 0, 2)
        mul_q(0, 0, 3)
        scale_x(4)
        scale_x(6)
        mm_p(0, 0, 0, 0)
        act_p(0, 1, 0, 1)
        act_p(0, 1, 0, 2)
        act_p(0, 1, 0, 3)
        act_p(1, 0, 0, 0)
        act_p(1, 1, 0, 2)
        turn_y(0, 1, 0)
        take_y(0, 1, 0, "S")
        turn_y(1, 1, 0)
        take_y(1, 1, 0, "S")
        scale_x(7)
        mm_p(0, 0, 0, 1)
        mm_p(1, 1, 0, 0)
        act_p(1, 0, 0, 2)
        quant_y(0, 1)
        turn_x(6)
        take_x(6, "V")
        mm_p(1, 0, 0, 1)
        act_p(0, 0, 0, 0)
        act_p(1, 1, 0, 0)
        mm_p(0, 1, 0, 0)
        mm_p(1, 1, 0, 3)
        mul_q(0, 0, 2)
        mul_q(1, 0, 2)
        act_p(0, 0, 0, 1)
        act_p(1, 0, 0, 1)
        mul_q(0, 0, 0)
        quant_y(1, 1)
        mm_g(0, 0, 0)
        mm_p(0, 1, 1, 0)
        mm_p(0, 1, 1, 1)
        mm_p(1, 1, 0, 1)
        act_p(0, 1, 0, 0)
        act_p(1, 1, 0, 3)
        mul_q(0, 0, 1)
        mul_q(1, 0, 0)
        add_w(0, 0, 0)
        turn_y(1, 2, 0)
        take_y(1, 2, 0, "S")
        mm_p(1, 1, 1, 0)
        mm_p(1, 1, 1, 1)
        act_p(1, 1, 0, 1)
        quant_y(1, 2)
        mm_p(0, 0, 1, 0)
        act_p(1, 1, 1, 0)
        act_p(1, 1, 1, 1)
        mul_q(1, 0, 3)
        turn_x(7)
        take_x(7, "S")
        mm_g(0, 0, 3)
        mm_g(1, 0, 1)
        act_p(0, 0, 1, 0)
        act_p(0, 1, 1, 0)
        act_p(0, 1, 1, 1)
        mul_q(1, 0, 1)
        add_w(0, 0, 3)
        add_w(1, 0, 1)
        turn_y(0, 2, 0)
        take_y(0, 2, 0, "S")
        mm_g(0, 0, 1)
        mm_g(1, 0, 2)
        mm_g(1, 0, 3)
        mm_p(0, 0, 1, 1)
        mm_p(1, 0, 1, 1)
        act_p(1, 0, 1, 1)
        add_w(0, 0, 1)
        add_w(1, 0, 2)
        add_w(1, 0, 3)
        quant_y(0, 2)
        mm_g(0, 0, 2)
        mm_g(1, 0, 0)
        mm_p(1, 0, 1, 0)
        act_p(0, 0, 1, 1)
        act_p(1, 0, 1, 0)
        mul_q(1, 1, 0)
        add_w(0, 0, 2)
        add_w(1, 0, 0)
        turn_x(0)
        take_x(0, "S")
        turn_x(1)
        take_x(1, "S")
        mm_p(0, 1, 2, 1)
        mm_p(1, 1, 2, 0)
        act_p(0, 1, 2, 1)
        mul_q(0, 1, 1)
        mm_p(0, 1, 2, 0)
        mm_p(1, 0, 2, 0)
        act_p(0, 1, 2, 0)
        quant_w(0, 0)
        turn_x(2)
        take_x(2, "S")
        turn_x(3)
        take_x(3, "S")
        mm_g(0, 1, 0)
        mm_p(0, 0, 2, 1)
        mm_p(1, 0, 2, 1)
        act_p(1, 0, 2, 0)
        mul_q(0, 1, 0)
        mul_q(1, 1, 1)
        add_w(0, 1, 0)
        turn_x(5)
        take_x(5, "S")
        quant_x(0)
        mm_g(1, 1, 0)
        mm_p(0, 0, 2, 0)
        mm_p(1, 1, 2, 1)
        act_p(0, 0, 2, 1)
        act_p(1, 1, 2, 0)
        add_w(1, 1, 0)
        quant_w(1, 0)
        turn_x(4)
        take_x(4, "S")
        quant_x(1)
        mm_g(0, 1, 1)
        mm_g(1, 1, 1)
        act_p(0, 0, 2, 0)
        act_p(1, 0, 2, 1)
        act_p(1, 1, 2, 1)
        mul_q(0, 2, 0)
        mul_q(1, 2, 1)
        add_w(0, 1, 1)
        add_w(1, 1, 1)
        quant_w(0, 1)
        quant_w(1, 1)
        mm_g(0, 2, 0)
        mm_g(1, 2, 0)
        mm_out(0, 1)
        take_out(0, 1, "S")
        mm_out(0, 3)
        take_out(0, 3, "S")
        mm_out(0, 4)
        take_out(0, 4, "S")
        mul_q(0, 2, 1)
        mul_q(1, 2, 0)
        add_w(0, 2, 0)
        add_w(1, 2, 0)
        quant_w(0, 2)
        quant_w(1, 2)
        mm_out(0, 0)
        take_out(0, 0, "S")
        mm_out(0, 2)
        take_out(0, 2, "S")
        mm_out(0, 5)
        take_out(0, 5, "S")
        mm_out(0, 7)
        take_out(0, 7, "S")
        mm_g(0, 2, 1)
        mm_g(1, 2, 1)
        mm_out(0, 6)
        take_out(0, 6, "S")
        mm_out(1, 1)
        take_out(1, 1, "S")
        mm_out(1, 2)
        take_out(1, 2, "S")
        add_w(0, 2, 1)
        add_w(1, 2, 1)
        quant_w(0, 3)
        quant_w(1, 3)
        mm_out(1, 0)
        take_out(1, 0, "S")
        mm_out(1, 3)
        take_out(1, 3, "S")
        mm_out(2, 0)
        take_out(2, 0, "S")
        mm_out(2, 1)
        take_out(2, 1, "V")
        mm_out(3, 0)
        take_out(3, 0, "S")
        mm_out(3, 1)
        take_out(3, 1, "S")
